import numpy as np
import ml_dtypes


def mxq(x, axis, fmt="e4m3"):
    dtype, down = {"e4m3": (ml_dtypes.float8_e4m3fn, 7), "e5m2": (ml_dtypes.float8_e5m2, 14)}[fmt]
    v = np.moveaxis(np.asarray(x, np.float32).astype(ml_dtypes.bfloat16).astype(np.float64), axis, -1)
    blocks = v.reshape(v.shape[:-1] + (-1, 32))
    amax = np.abs(blocks).max(-1, keepdims=True)
    byte = np.maximum(np.where(amax > 0, np.frexp(amax)[1] - 1 + 127, 0) - down, 1)
    scale = np.exp2(byte - 127.0)
    codes = (blocks / scale).astype(np.float32).astype(dtype).astype(np.float64)
    return np.moveaxis((codes * scale).reshape(v.shape), -1, axis)


WIDE = False


def mx_kscale(k):
    if not WIDE:
        return np.ones(k)
    levels = np.array([18, -18])
    if k % 512:
        return np.exp2(np.random.permutation(np.resize(levels, k // 32))).repeat(32)
    a = np.empty((k // 512, 16))
    for p in range(k // 512):
        a[p, :8] = np.random.permutation(np.resize(levels, 8))
        for g in range(8):
            far = levels[np.abs(levels - a[p, g]) >= 10]
            a[p, g + 8] = far[np.random.randint(len(far))]
    return np.exp2(a.ravel()).repeat(32)


def f64(x):
    return np.asarray(x).astype(np.float64)


def striped(idx):
    return np.tile(np.asarray(idx).reshape(-1, 16).T, (8, 1)).astype(np.uint16)


def unstriped(offs):
    return offs[:16].T.reshape(-1).astype(np.int64)


T, C, D, DV = 1024, 512, 512, 512
BETA = 0.25


def setup_inputs():
    n = np.random.standard_normal
    grid = lambda v: np.clip(np.round(v * 16) / 16, -4, 4)
    u = mx_kscale(T)
    return {
        "zT": (grid(n((DV, T)))).astype(np.float32),
        "cb": (grid(n((DV, C)))).astype(np.float32),
        "dyT": (grid(0.5 * n((DV, T)))).astype(np.float32),
        "tw": np.tile(np.random.randint(8, 33, T) / 16.0 * u, (128, 1)).astype(np.float32),
        "xT": (n((D, T)) / np.sqrt(T) / u).astype(np.float32),
        "offs": striped(np.random.randint(0, C, T)),
    }


def reference(zT, cb, dyT, tw, xT, offs):
    e = f64(zT) - f64(cb)[:, unstriped(offs)]
    g = f64(tw)[:1] * (f64(dyT) + BETA * e)
    return mxq(f64(xT), 1, "e4m3") @ mxq(g, 1, "e5m2").T

@@ -1,0 +1,194 @@
+from contextlib import ExitStack
+
+import concourse.mybir as mybir
+from concourse.masks import make_identity
+
+T, C, D, DV = 1024, 512, 512, 512
+BETA = 0.25
+FLOPS = 2 * D * DV * T
+
+F32 = mybir.dt.float32
+BF16 = mybir.dt.bfloat16
+U32 = mybir.dt.uint32
+U16 = mybir.dt.uint16
+U8 = mybir.dt.uint8
+E4M3X4 = mybir.dt.float8_e4m3fn_x4
+E5M2X4 = mybir.dt.float8_e5m2_x4
+MULT = mybir.AluOpType.mult
+
+P = 128
+PACK = 4
+K_PASS = P * PACK
+PASSES = T // K_PASS
+G_BLOCKS = DV // P
+X_BLOCKS = D // P
+WINDOW = K_PASS + 16
+LIST_COLS = K_PASS // 16
+X_ON_SCALAR = 2
+
+
+def tile_attend_gvq_s_w_kernel(tc, zT, cb, dyT, tw, xT, offs, out):
+    nc = tc.nc
+    with ExitStack() as ctx:
+        keep = ctx.enter_context(tc.tile_pool(name="keep", bufs=1))
+        turn = ctx.enter_context(tc.psum_pool(name="turn", bufs=6))
+        sums = ctx.enter_context(tc.psum_pool(name="sums", bufs=2))
+
+        offsets = keep.tile([P, T // 16], U16, name="offsets")
+        books = [keep.tile([P, WINDOW], F32, name="book%d" % b) for b in range(G_BLOCKS)]
+        zs = [keep.tile([P, T], F32, name="z%d" % b) for b in range(G_BLOCKS)]
+        dys = [keep.tile([P, T], F32, name="dy%d" % b) for b in range(G_BLOCKS)]
+        xs = [keep.tile([P, T], F32, name="x%d" % b) for b in range(X_BLOCKS)]
+        weights = keep.tile([P, PASSES, PACK], F32, name="weights")
+
+        def rows(b):
+            return slice(b * P, (b + 1) * P)
+
+        def load_book(b):
+            nc.sync.dma_start(books[b][:, :C], cb[rows(b), :])
+
+        def load_z_dy(b):
+            nc.sync.dma_start(zs[b][:], zT[rows(b), :])
+            nc.sync.dma_start(dys[b][:], dyT[rows(b), :])
+
+        nc.sync.dma_start(offsets[:], offs)
+        load_book(0)
+        nc.scalar.dma_start(weights[:], tw[0, :].rearrange("(h p j) -> p h j", h=PASSES, j=PACK))
+        load_book(1)
+        load_z_dy(0)
+        load_book(2)
+        load_z_dy(1)
+        load_book(3)
+        load_z_dy(2)
+        nc.sync.dma_start(xs[0][:], xT[rows(0), :])
+        load_z_dy(3)
+        for b in range(1, X_BLOCKS - 1):
+            nc.sync.dma_start(xs[b][:], xT[rows(b), :])
+        for h in range(PASSES):
+            cols = slice(h * K_PASS, (h + 1) * K_PASS)
+            nc.sync.dma_start(xs[X_BLOCKS - 1][:, cols], xT[rows(X_BLOCKS - 1), cols])
+
+        ones = keep.tile([P, K_PASS], F32, name="ones")
+        minus_beta = keep.tile([P, K_PASS], F32, name="minus_beta")
+        nc.gpsimd.memset(ones[:], 1.0)
+        nc.scalar.mul(minus_beta[:], ones[:], -BETA)
+        for b in range(G_BLOCKS):
+            nc.gpsimd.memset(books[b][:, C:], 0.0)
+        ident = keep.tile([P, P], F32, name="ident")
+        make_identity(nc, ident[:])
+
+        picked = [keep.tile([P, T], F32, name="picked%d" % b) for b in range(G_BLOCKS)]
+        z_scaled = [keep.tile([P, PASSES, PACK, P], F32, name="z_scaled%d" % b) for b in range(G_BLOCKS)]
+        g_bf = keep.tile([P, G_BLOCKS, PASSES, P, PACK], BF16, name="g_bf", align_bytes=64)
+        g_codes = keep.tile([P, PASSES, DV], U32, name="g_codes", align_bytes=64)
+        g_scales = keep.tile([P, PASSES, DV], U8, name="g_scales", align_bytes=64)
+        x_pairs = [keep.tile([P, 2, PASSES * P, 2], BF16, name="x_pairs%d" % b) for b in range(X_BLOCKS)]
+        x_bf = keep.tile([P, X_BLOCKS, PASSES, P * PACK], BF16, name="x_bf", align_bytes=64)
+        x_codes = keep.tile([P, X_BLOCKS, PASSES, P], U32, name="x_codes", align_bytes=64)
+        x_scales = keep.tile([P, X_BLOCKS, PASSES, P], U8, name="x_scales", align_bytes=64)
+        results = [keep.tile([P, DV], F32, name="result%d" % b) for b in range(X_BLOCKS)]
+
+        def tokens(h):
+            return slice(h * K_PASS, (h + 1) * K_PASS)
+
+        def every_fourth(h, j):
+            return slice(h * K_PASS + j, (h + 1) * K_PASS, PACK)
+
+        def gather(b, h):
+            nc.vector.tensor_tensor(
+                picked[b][:, tokens(h)],
+                books[b][:].indirect(offsets[:, h * LIST_COLS : (h + 1) * LIST_COLS]),
+                minus_beta[:],
+                MULT,
+            )
+
+        def form_g(b, h):
+            nc.scalar.mul(
+                z_scaled[b][:, h].rearrange("n j p -> n p j"),
+                zs[b][:, tokens(h)].rearrange("n (p j) -> n p j", j=PACK),
+                BETA,
+            )
+            bank = turn.tile([P, PACK, P], F32, name="bank")
+            terms = (
+                [picked[b][:, every_fourth(h, j)] for j in range(PACK)],
+                [z_scaled[b][:, h, j, :] for j in range(PACK)],
+                [dys[b][:, every_fourth(h, j)] for j in range(PACK)],
+            )
+            for i in range(len(terms)):
+                for j in range(PACK):
+                    nc.tensor.matmul(
+                        bank[:, j, :],
+                        terms[i][j],
+                        ident[:],
+                        start=(i == 0 and j == 0),
+                        stop=(i == len(terms) - 1 and j == PACK - 1),
+                        is_transpose=True,
+                    )
+            nc.vector.tensor_tensor(
+                g_bf[:, b, h],
+                bank[:].rearrange("p j n -> p n j"),
+                weights[:, h, :].unsqueeze(1).to_broadcast([P, P, PACK]),
+                MULT,
+            )
+
+        def quantize_g(b, h):
+            nc.vector.quantize_mx(
+                out=g_codes[:, h, rows(b)].bitcast(E5M2X4),
+                scales=g_scales[:, h, rows(b)],
+                in_=g_bf[:, b, h].rearrange("p n j -> p (n j)"),
+            )
+
+        def form_x(b, h0, h1):
+            rounded = x_pairs[b][:, :, h0 * P : h1 * P, :].rearrange("m u p e -> m p u e")
+            raw = xs[b][:, h0 * K_PASS : h1 * K_PASS].rearrange("m (p u e) -> m p u e", u=2, e=2)
+            if b < X_ON_SCALAR:
+                nc.scalar.copy(rounded, raw)
+            else:
+                nc.vector.tensor_copy(rounded, raw)
+            words = x_pairs[b][:].rearrange("m u p e -> m (u p e)").bitcast(F32)
+            bank = turn.tile([P, h1 - h0, 2, P], F32, name="bank")
+            for h in range(h0, h1):
+                for u in range(2):
+                    first = (u * PASSES + h) * P
+                    nc.tensor.transpose(bank[:, h - h0, u, :], words[:, first : first + P], ident[:])
+            grouped = x_bf[:, b, h0:h1, :].rearrange("p h k -> p (h k)").bitcast(F32)
+            nc.scalar.copy(
+                grouped.rearrange("p (h m u) -> p h m u", m=P, u=2),
+                bank[:].rearrange("p h u m -> p h m u"),
+            )
+            nc.vector.quantize_mx(
+                out=x_codes[:, b, h0:h1, :].rearrange("p h m -> p (h m)").bitcast(E4M3X4),
+                scales=x_scales[:, b, h0:h1, :].rearrange("p h m -> p (h m)"),
+                in_=x_bf[:, b, h0:h1, :].rearrange("p h k -> p (h k)"),
+            )
+
+        for b in range(G_BLOCKS):
+            for h in range(PASSES):
+                gather(b, h)
+            for h in range(PASSES):
+                form_g(b, h)
+            for h in range(PASSES):
+                quantize_g(b, h)
+
+        for b in range(X_BLOCKS):
+            if b < X_BLOCKS - 1:
+                form_x(b, 0, PASSES)
+            else:
+                for h in range(PASSES):
+                    form_x(b, h, h + 1)
+            acc = sums.tile([P, DV], F32, name="acc")
+            for h in range(PASSES):
+                nc.tensor.matmul_mx(
+                    out=acc[:],
+                    lhsT=x_codes[:, b, h, :].bitcast(E4M3X4),
+                    lhsT_scale=x_scales[:, b, h, :],
+                    rhs=g_codes[:, h, :].bitcast(E5M2X4),
+                    rhs_scale=g_scales[:, h, :],
+                    start=(h == 0),
+                    stop=(h == PASSES - 1),
+                )
+            if b % 2 == 0:
+                nc.scalar.copy(results[b][:], acc[:])
+            else:
+                nc.vector.tensor_copy(results[b][:], acc[:])
+            nc.sync.dma_start(out[rows(b), :], results[b][:])

@@ -15,6 +15,7 @@ U8 = mybir.dt.uint8
 E4M3X4 = mybir.dt.float8_e4m3fn_x4
 E5M2X4 = mybir.dt.float8_e5m2_x4
 MULT = mybir.AluOpType.mult
+ADD = mybir.AluOpType.add
 
 P = 128
 PACK = 4
@@ -22,24 +23,27 @@ K_PASS = P * PACK
 PASSES = T // K_PASS
 G_BLOCKS = DV // P
 X_BLOCKS = D // P
-WINDOW = K_PASS + 16
+WINDOW = 704
 LIST_COLS = K_PASS // 16
-X_ON_SCALAR = 2
+RUN = 8
 
 
 def tile_attend_gvq_s_w_kernel(tc, zT, cb, dyT, tw, xT, offs, out):
     nc = tc.nc
     with ExitStack() as ctx:
         keep = ctx.enter_context(tc.tile_pool(name="keep", bufs=1))
-        turn = ctx.enter_context(tc.psum_pool(name="turn", bufs=6))
-        sums = ctx.enter_context(tc.psum_pool(name="sums", bufs=2))
+        g_turn = ctx.enter_context(tc.psum_pool(name="g_turn", bufs=3))
+        x_turn = ctx.enter_context(tc.psum_pool(name="x_turn", bufs=2))
+        sums = ctx.enter_context(tc.psum_pool(name="sums", bufs=3))
 
         offsets = keep.tile([P, T // 16], U16, name="offsets")
         books = [keep.tile([P, WINDOW], F32, name="book%d" % b) for b in range(G_BLOCKS)]
         zs = [keep.tile([P, T], F32, name="z%d" % b) for b in range(G_BLOCKS)]
         dys = [keep.tile([P, T], F32, name="dy%d" % b) for b in range(G_BLOCKS)]
         xs = [keep.tile([P, T], F32, name="x%d" % b) for b in range(X_BLOCKS)]
+        tw_rows = keep.tile([P, P], F32, name="tw_rows")
         weights = keep.tile([P, PASSES, PACK], F32, name="weights")
+        nc.gpsimd.memset(tw_rows[:], 0.0)
 
         def rows(b):
             return slice(b * P, (b + 1) * P)
@@ -53,7 +57,11 @@ def tile_attend_gvq_s_w_kernel(tc, zT, cb, dyT, tw, xT, offs, out):
 
         nc.sync.dma_start(offsets[:], offs)
         load_book(0)
-        nc.scalar.dma_start(weights[:], tw[0, :].rearrange("(h p j) -> p h j", h=PASSES, j=PACK))
+        for h in range(PASSES):
+            nc.scalar.dma_start(
+                tw_rows[h * PACK : (h + 1) * PACK, :].rearrange("j (g i) -> j g i", i=RUN),
+                tw[0, h * K_PASS : (h + 1) * K_PASS].rearrange("(g j i) -> j g i", j=PACK, i=RUN),
+            )
         load_book(1)
         load_z_dy(0)
         load_book(2)
@@ -68,17 +76,18 @@ def tile_attend_gvq_s_w_kernel(tc, zT, cb, dyT, tw, xT, offs, out):
             cols = slice(h * K_PASS, (h + 1) * K_PASS)
             nc.sync.dma_start(xs[X_BLOCKS - 1][:, cols], xT[rows(X_BLOCKS - 1), cols])
 
-        ones = keep.tile([P, K_PASS], F32, name="ones")
-        minus_beta = keep.tile([P, K_PASS], F32, name="minus_beta")
-        nc.gpsimd.memset(ones[:], 1.0)
-        nc.scalar.mul(minus_beta[:], ones[:], -BETA)
         for b in range(G_BLOCKS):
             nc.gpsimd.memset(books[b][:, C:], 0.0)
         ident = keep.tile([P, P], F32, name="ident")
         make_identity(nc, ident[:])
 
-        picked = [keep.tile([P, T], F32, name="picked%d" % b) for b in range(G_BLOCKS)]
+        tw_bank = x_turn.tile([P, P], F32, name="x_bank")
+        nc.tensor.transpose(tw_bank[:], tw_rows[:], ident[:])
+        nc.scalar.mul(weights[:].rearrange("p h j -> p (h j)"), tw_bank[:, : PASSES * PACK], -BETA)
+
+        picked = [keep.tile([P, PASSES, PACK, P], F32, name="picked%d" % b) for b in range(G_BLOCKS)]
         z_scaled = [keep.tile([P, PASSES, PACK, P], F32, name="z_scaled%d" % b) for b in range(G_BLOCKS)]
+        dy_scaled = [keep.tile([P, PASSES, PACK, P], F32, name="dy_scaled%d" % b) for b in range(G_BLOCKS)]
         g_bf = keep.tile([P, G_BLOCKS, PASSES, P, PACK], BF16, name="g_bf", align_bytes=64)
         g_codes = keep.tile([P, PASSES, DV], U32, name="g_codes", align_bytes=64)
         g_scales = keep.tile([P, PASSES, DV], U8, name="g_scales", align_bytes=64)
@@ -91,29 +100,24 @@ def tile_attend_gvq_s_w_kernel(tc, zT, cb, dyT, tw, xT, offs, out):
         def tokens(h):
             return slice(h * K_PASS, (h + 1) * K_PASS)
 
-        def every_fourth(h, j):
-            return slice(h * K_PASS + j, (h + 1) * K_PASS, PACK)
+        def in_token_order(planes):
+            return planes.rearrange("n j (g i) -> n g j i", i=RUN)
 
         def gather(b, h):
-            nc.vector.tensor_tensor(
-                picked[b][:, tokens(h)],
-                books[b][:].indirect(offsets[:, h * LIST_COLS : (h + 1) * LIST_COLS]),
-                minus_beta[:],
-                MULT,
+            nc.vector.tensor_copy(
+                in_token_order(picked[b][:, h].bitcast(U32)),
+                books[b][:].bitcast(U32).indirect(offsets[:, h * LIST_COLS : (h + 1) * LIST_COLS]),
             )
 
         def form_g(b, h):
-            nc.scalar.mul(
-                z_scaled[b][:, h].rearrange("n j p -> n p j"),
-                zs[b][:, tokens(h)].rearrange("n (p j) -> n p j", j=PACK),
-                BETA,
-            )
-            bank = turn.tile([P, PACK, P], F32, name="bank")
-            terms = (
-                [picked[b][:, every_fourth(h, j)] for j in range(PACK)],
-                [z_scaled[b][:, h, j, :] for j in range(PACK)],
-                [dys[b][:, every_fourth(h, j)] for j in range(PACK)],
-            )
+            for planes, raw, factor in ((z_scaled, zs, -1.0), (dy_scaled, dys, -1.0 / BETA)):
+                nc.scalar.mul(
+                    in_token_order(planes[b][:, h]),
+                    raw[b][:, tokens(h)].rearrange("n (g j i) -> n g j i", j=PACK, i=RUN),
+                    factor,
+                )
+            bank = g_turn.tile([P, PACK, P], F32, name="g_bank")
+            terms = [[planes[b][:, h, j, :] for j in range(PACK)] for planes in (picked, z_scaled, dy_scaled)]
             for i in range(len(terms)):
                 for j in range(PACK):
                     nc.tensor.matmul(
@@ -139,14 +143,15 @@ def tile_attend_gvq_s_w_kernel(tc, zT, cb, dyT, tw, xT, offs, out):
             )
 
         def form_x(b, h0, h1):
-            rounded = x_pairs[b][:, :, h0 * P : h1 * P, :].rearrange("m u p e -> m p u e")
-            raw = xs[b][:, h0 * K_PASS : h1 * K_PASS].rearrange("m (p u e) -> m p u e", u=2, e=2)
-            if b < X_ON_SCALAR:
-                nc.scalar.copy(rounded, raw)
-            else:
-                nc.vector.tensor_copy(rounded, raw)
+            for u in range(2):
+                rounded = x_pairs[b][:, u, h0 * P : h1 * P, :].rearrange("m (g i) e -> m g i e", i=RUN)
+                raw = xs[b][:, h0 * K_PASS : h1 * K_PASS].rearrange("m (g u e i) -> m u g i e", u=2, e=2, i=RUN)
+                if b < X_BLOCKS - 1:
+                    nc.gpsimd.tensor_scalar(rounded, raw[:, u], 1.0, 0.0, MULT, ADD)
+                else:
+                    nc.vector.tensor_copy(rounded, raw[:, u])
             words = x_pairs[b][:].rearrange("m u p e -> m (u p e)").bitcast(F32)
-            bank = turn.tile([P, h1 - h0, 2, P], F32, name="bank")
+            bank = x_turn.tile([P, h1 - h0, 2, P], F32, name="x_bank")
             for h in range(h0, h1):
                 for u in range(2):
                     first = (u * PASSES + h) * P
@@ -162,9 +167,12 @@ def tile_attend_gvq_s_w_kernel(tc, zT, cb, dyT, tw, xT, offs, out):
                 in_=x_bf[:, b, h0:h1, :].rearrange("p h k -> p (h k)"),
             )
 
+        for h in range(PASSES):
+            gather(0, h)
         for b in range(G_BLOCKS):
-            for h in range(PASSES):
-                gather(b, h)
+            if b + 1 < G_BLOCKS:
+                for h in range(PASSES):
+                    gather(b + 1, h)
             for h in range(PASSES):
                 form_g(b, h)
             for h in range(PASSES):
@@ -187,7 +195,7 @@ def tile_attend_gvq_s_w_kernel(tc, zT, cb, dyT, tw, xT, offs, out):
                     start=(h == 0),
                     stop=(h == PASSES - 1),
                 )
-            if b % 2 == 0:
+            if b != 1:
                 nc.scalar.copy(results[b][:], acc[:])
             else:
                 nc.vector.tensor_copy(results[b][:], acc[:])

@@ -15,7 +15,6 @@ U8 = mybir.dt.uint8
 E4M3X4 = mybir.dt.float8_e4m3fn_x4
 E5M2X4 = mybir.dt.float8_e5m2_x4
 MULT = mybir.AluOpType.mult
-ADD = mybir.AluOpType.add
 
 P = 128
 PACK = 4
@@ -32,9 +31,8 @@ def tile_attend_gvq_s_w_kernel(tc, zT, cb, dyT, tw, xT, offs, out):
     nc = tc.nc
     with ExitStack() as ctx:
         keep = ctx.enter_context(tc.tile_pool(name="keep", bufs=1))
-        g_turn = ctx.enter_context(tc.psum_pool(name="g_turn", bufs=3))
+        banks = ctx.enter_context(tc.psum_pool(name="banks", bufs=6))
         x_turn = ctx.enter_context(tc.psum_pool(name="x_turn", bufs=2))
-        sums = ctx.enter_context(tc.psum_pool(name="sums", bufs=3))
 
         offsets = keep.tile([P, T // 16], U16, name="offsets")
         books = [keep.tile([P, WINDOW], F32, name="book%d" % b) for b in range(G_BLOCKS)]
@@ -88,10 +86,9 @@ def tile_attend_gvq_s_w_kernel(tc, zT, cb, dyT, tw, xT, offs, out):
         picked = [keep.tile([P, PASSES, PACK, P], F32, name="picked%d" % b) for b in range(G_BLOCKS)]
         z_scaled = [keep.tile([P, PASSES, PACK, P], F32, name="z_scaled%d" % b) for b in range(G_BLOCKS)]
         dy_scaled = [keep.tile([P, PASSES, PACK, P], F32, name="dy_scaled%d" % b) for b in range(G_BLOCKS)]
-        g_bf = keep.tile([P, G_BLOCKS, PASSES, P, PACK], BF16, name="g_bf", align_bytes=64)
+        g_bf = keep.tile([P, PASSES, G_BLOCKS, P, PACK], BF16, name="g_bf", align_bytes=64)
         g_codes = keep.tile([P, PASSES, DV], U32, name="g_codes", align_bytes=64)
         g_scales = keep.tile([P, PASSES, DV], U8, name="g_scales", align_bytes=64)
-        x_pairs = [keep.tile([P, 2, PASSES * P, 2], BF16, name="x_pairs%d" % b) for b in range(X_BLOCKS)]
         x_bf = keep.tile([P, X_BLOCKS, PASSES, P * PACK], BF16, name="x_bf", align_bytes=64)
         x_codes = keep.tile([P, X_BLOCKS, PASSES, P], U32, name="x_codes", align_bytes=64)
         x_scales = keep.tile([P, X_BLOCKS, PASSES, P], U8, name="x_scales", align_bytes=64)
@@ -116,7 +113,7 @@ def tile_attend_gvq_s_w_kernel(tc, zT, cb, dyT, tw, xT, offs, out):
                     raw[b][:, tokens(h)].rearrange("n (g j i) -> n g j i", j=PACK, i=RUN),
                     factor,
                 )
-            bank = g_turn.tile([P, PACK, P], F32, name="g_bank")
+            bank = banks.tile([P, PACK, P], F32, name="bank")
             terms = [[planes[b][:, h, j, :] for j in range(PACK)] for planes in (picked, z_scaled, dy_scaled)]
             for i in range(len(terms)):
                 for j in range(PACK):
@@ -129,74 +126,94 @@ def tile_attend_gvq_s_w_kernel(tc, zT, cb, dyT, tw, xT, offs, out):
                         is_transpose=True,
                     )
             nc.vector.tensor_tensor(
-                g_bf[:, b, h],
+                g_bf[:, h, b],
                 bank[:].rearrange("p j n -> p n j"),
                 weights[:, h, :].unsqueeze(1).to_broadcast([P, P, PACK]),
                 MULT,
             )
 
-        def quantize_g(b, h):
+        def quantize_g(b0, b1, h):
             nc.vector.quantize_mx(
-                out=g_codes[:, h, rows(b)].bitcast(E5M2X4),
-                scales=g_scales[:, h, rows(b)],
-                in_=g_bf[:, b, h].rearrange("p n j -> p (n j)"),
+                out=g_codes[:, h, b0 * P : b1 * P].bitcast(E5M2X4),
+                scales=g_scales[:, h, b0 * P : b1 * P],
+                in_=g_bf[:, h, b0:b1].rearrange("p b n j -> p (b n j)"),
             )
 
-        def form_x(b, h0, h1):
+        def form_x(b, h0, h1, words, on_scalar):
+            pairs = words.bitcast(BF16).rearrange("m (u g i e) -> m u g i e", u=2, i=RUN, e=2)
+            raw = xs[b][:, h0 * K_PASS : h1 * K_PASS].rearrange("m (g u e i) -> m u g i e", u=2, e=2, i=RUN)
             for u in range(2):
-                rounded = x_pairs[b][:, u, h0 * P : h1 * P, :].rearrange("m (g i) e -> m g i e", i=RUN)
-                raw = xs[b][:, h0 * K_PASS : h1 * K_PASS].rearrange("m (g u e i) -> m u g i e", u=2, e=2, i=RUN)
-                if b < X_BLOCKS - 1:
-                    nc.gpsimd.tensor_scalar(rounded, raw[:, u], 1.0, 0.0, MULT, ADD)
+                if on_scalar:
+                    nc.scalar.copy(pairs[:, u], raw[:, u])
                 else:
-                    nc.vector.tensor_copy(rounded, raw[:, u])
-            words = x_pairs[b][:].rearrange("m u p e -> m (u p e)").bitcast(F32)
+                    nc.vector.tensor_copy(pairs[:, u], raw[:, u])
             bank = x_turn.tile([P, h1 - h0, 2, P], F32, name="x_bank")
-            for h in range(h0, h1):
+            for h in range(h1 - h0):
                 for u in range(2):
-                    first = (u * PASSES + h) * P
-                    nc.tensor.transpose(bank[:, h - h0, u, :], words[:, first : first + P], ident[:])
+                    first = (u * (h1 - h0) + h) * P
+                    nc.tensor.transpose(bank[:, h, u, :], words[:, first : first + P], ident[:])
             grouped = x_bf[:, b, h0:h1, :].rearrange("p h k -> p (h k)").bitcast(F32)
             nc.scalar.copy(
                 grouped.rearrange("p (h m u) -> p h m u", m=P, u=2),
                 bank[:].rearrange("p h u m -> p h m u"),
             )
+
+        def quantize_x(b, h0, h1):
             nc.vector.quantize_mx(
                 out=x_codes[:, b, h0:h1, :].rearrange("p h m -> p (h m)").bitcast(E4M3X4),
                 scales=x_scales[:, b, h0:h1, :].rearrange("p h m -> p (h m)"),
                 in_=x_bf[:, b, h0:h1, :].rearrange("p h k -> p (h k)"),
             )
 
-        for h in range(PASSES):
-            gather(0, h)
-        for b in range(G_BLOCKS):
-            if b + 1 < G_BLOCKS:
-                for h in range(PASSES):
-                    gather(b + 1, h)
-            for h in range(PASSES):
-                form_g(b, h)
-            for h in range(PASSES):
-                quantize_g(b, h)
+        def multiply(acc, b, h):
+            nc.tensor.matmul_mx(
+                out=acc[:],
+                lhsT=x_codes[:, b, h, :].bitcast(E4M3X4),
+                lhsT_scale=x_scales[:, b, h, :],
+                rhs=g_codes[:, h, :].bitcast(E5M2X4),
+                rhs_scale=g_scales[:, h, :],
+                start=(h == 0),
+                stop=(h == PASSES - 1),
+            )
 
+        x0_words = keep.tile([P, PACK * P], F32, name="x0_words")
+
+        for b in (0, 1):
+            gather(b, 0)
+            gather(b, 1)
+        form_g(0, 0)
+        form_g(0, 1)
+        gather(2, 0)
+        gather(2, 1)
+        form_g(1, 0)
+        form_g(1, 1)
+        quantize_g(0, 2, 0)
+        gather(3, 0)
+        quantize_g(0, 2, 1)
+        gather(3, 1)
+        form_g(2, 0)
+        form_g(3, 0)
+        form_x(0, 0, PASSES, x0_words[:], True)
+        quantize_x(0, 0, PASSES)
+        quantize_g(2, 4, 0)
+        form_g(2, 1)
+        form_g(3, 1)
+        for b in (1, 2):
+            form_x(b, 0, PASSES, picked[3][:, b - 1].rearrange("n j p -> n (j p)"), True)
+        quantize_x(1, 0, PASSES)
+        for h in range(PASSES):
+            form_x(3, h, h + 1, g_bf[:, 0, 2 + h].rearrange("p n j -> p (n j)").bitcast(F32), False)
+        quantize_g(2, 4, 1)
+        quantize_x(2, 0, PASSES)
+        for h in range(PASSES):
+            quantize_x(3, h, h + 1)
+        accs = [banks.tile([P, DV], F32, name="bank") for b in range(X_BLOCKS)]
         for b in range(X_BLOCKS):
-            if b < X_BLOCKS - 1:
-                form_x(b, 0, PASSES)
+            multiply(accs[b], b, 0)
+        for b in range(X_BLOCKS):
+            multiply(accs[b], b, 1)
+            if b % 2 == 0:
+                nc.scalar.copy(results[b][:], accs[b][:])
             else:
-                for h in range(PASSES):
-                    form_x(b, h, h + 1)
-            acc = sums.tile([P, DV], F32, name="acc")
-            for h in range(PASSES):
-                nc.tensor.matmul_mx(
-                    out=acc[:],
-                    lhsT=x_codes[:, b, h, :].bitcast(E4M3X4),
-                    lhsT_scale=x_scales[:, b, h, :],
-                    rhs=g_codes[:, h, :].bitcast(E5M2X4),
-                    rhs_scale=g_scales[:, h, :],
-                    start=(h == 0),
-                    stop=(h == PASSES - 1),
-                )
-            if b != 1:
-                nc.scalar.copy(results[b][:], acc[:])
-            else:
-                nc.vector.tensor_copy(results[b][:], acc[:])
+                nc.vector.tensor_copy(results[b][:], accs[b][:])
             nc.sync.dma_start(out[rows(b), :], results[b][:])

@@ -20,139 +20,140 @@ P = 128
 PACK = 4
 K_PASS = P * PACK
 PASSES = T // K_PASS
-G_BLOCKS = DV // P
-X_BLOCKS = D // P
-WINDOW = 704
+BLOCKS = DV // P
+LAST = BLOCKS - 1
 LIST_COLS = K_PASS // 16
-RUN = 8
+WINDOW = C + 16
+X_BANKS = 2
+G_BANKS = 8 - X_BANKS
 
 
 def tile_attend_gvq_s_w_kernel(tc, zT, cb, dyT, tw, xT, offs, out):
     nc = tc.nc
     with ExitStack() as ctx:
         keep = ctx.enter_context(tc.tile_pool(name="keep", bufs=1))
-        banks = ctx.enter_context(tc.psum_pool(name="banks", bufs=6))
-        x_turn = ctx.enter_context(tc.psum_pool(name="x_turn", bufs=2))
+        banks = ctx.enter_context(tc.psum_pool(name="banks", bufs=G_BANKS))
+        x_turn = ctx.enter_context(tc.psum_pool(name="x_turn", bufs=X_BANKS))
 
         offsets = keep.tile([P, T // 16], U16, name="offsets")
-        books = [keep.tile([P, WINDOW], F32, name="book%d" % b) for b in range(G_BLOCKS)]
-        zs = [keep.tile([P, T], F32, name="z%d" % b) for b in range(G_BLOCKS)]
-        dys = [keep.tile([P, T], F32, name="dy%d" % b) for b in range(G_BLOCKS)]
-        xs = [keep.tile([P, T], F32, name="x%d" % b) for b in range(X_BLOCKS)]
-        tw_rows = keep.tile([P, P], F32, name="tw_rows")
-        weights = keep.tile([P, PASSES, PACK], F32, name="weights")
-        nc.gpsimd.memset(tw_rows[:], 0.0)
+        books = [keep.tile([P, WINDOW], F32, name="book%d" % b) for b in range(BLOCKS)]
+        zs = [keep.tile([P, T], F32, name="z%d" % b) for b in range(BLOCKS)]
+        dys = [keep.tile([P, T], F32, name="dy%d" % b) for b in range(BLOCKS)]
+        xs = [keep.tile([P, T], F32, name="x%d" % b) for b in range(BLOCKS)]
+        tw_words = keep.tile([P, PASSES, PACK], F32, name="tw_words")
 
         def rows(b):
             return slice(b * P, (b + 1) * P)
 
+        def tokens(h):
+            return slice(h * K_PASS, (h + 1) * K_PASS)
+
+        def plane(h, j):
+            return slice(h * K_PASS + j, (h + 1) * K_PASS, PACK)
+
         def load_book(b):
             nc.sync.dma_start(books[b][:, :C], cb[rows(b), :])
 
-        def load_z_dy(b):
-            nc.sync.dma_start(zs[b][:], zT[rows(b), :])
-            nc.sync.dma_start(dys[b][:], dyT[rows(b), :])
-
         nc.sync.dma_start(offsets[:], offs)
         load_book(0)
-        for h in range(PASSES):
-            nc.scalar.dma_start(
-                tw_rows[h * PACK : (h + 1) * PACK, :].rearrange("j (g i) -> j g i", i=RUN),
-                tw[0, h * K_PASS : (h + 1) * K_PASS].rearrange("(g j i) -> j g i", j=PACK, i=RUN),
-            )
         load_book(1)
-        load_z_dy(0)
-        load_book(2)
-        load_z_dy(1)
-        load_book(3)
-        load_z_dy(2)
-        nc.sync.dma_start(xs[0][:], xT[rows(0), :])
-        load_z_dy(3)
-        for b in range(1, X_BLOCKS - 1):
-            nc.sync.dma_start(xs[b][:], xT[rows(b), :])
+        nc.sync.dma_start(tw_words[:], tw[0, :].rearrange("(h p j) -> p h j", h=PASSES, j=PACK))
+        for b in range(BLOCKS):
+            nc.sync.dma_start(zs[b][:], zT[rows(b), :])
+            nc.sync.dma_start(dys[b][:], dyT[rows(b), :])
+            if b + 2 < BLOCKS:
+                load_book(b + 2)
+            if b >= 1:
+                nc.sync.dma_start(xs[b - 1][:], xT[rows(b - 1), :])
         for h in range(PASSES):
-            cols = slice(h * K_PASS, (h + 1) * K_PASS)
-            nc.sync.dma_start(xs[X_BLOCKS - 1][:, cols], xT[rows(X_BLOCKS - 1), cols])
+            nc.sync.dma_start(xs[LAST][:, tokens(h)], xT[rows(LAST), tokens(h)])
 
-        for b in range(G_BLOCKS):
+        ones = keep.tile([P, K_PASS], F32, name="ones")
+        minus_beta = keep.tile([P, K_PASS], F32, name="minus_beta")
+        nc.gpsimd.memset(ones[:], 1.0)
+        nc.scalar.mul(minus_beta[:], ones[:], -BETA)
+        for b in range(BLOCKS):
             nc.gpsimd.memset(books[b][:, C:], 0.0)
         ident = keep.tile([P, P], F32, name="ident")
         make_identity(nc, ident[:])
 
-        tw_bank = x_turn.tile([P, P], F32, name="x_bank")
-        nc.tensor.transpose(tw_bank[:], tw_rows[:], ident[:])
-        nc.scalar.mul(weights[:].rearrange("p h j -> p (h j)"), tw_bank[:, : PASSES * PACK], -BETA)
+        weights = keep.tile([P, PASSES, P, PACK], F32, name="weights")
+        for h in range(PASSES):
+            nc.scalar.copy(weights[:, h], tw_words[:, h, :].unsqueeze(1).to_broadcast([P, P, PACK]))
 
-        picked = [keep.tile([P, PASSES, PACK, P], F32, name="picked%d" % b) for b in range(G_BLOCKS)]
-        z_scaled = [keep.tile([P, PASSES, PACK, P], F32, name="z_scaled%d" % b) for b in range(G_BLOCKS)]
-        dy_scaled = [keep.tile([P, PASSES, PACK, P], F32, name="dy_scaled%d" % b) for b in range(G_BLOCKS)]
-        g_bf = keep.tile([P, PASSES, G_BLOCKS, P, PACK], BF16, name="g_bf", align_bytes=64)
+        picked = [keep.tile([P, T], F32, name="picked%d" % b) for b in range(BLOCKS)]
+        z_planes = [keep.tile([P, PASSES, PACK, P], F32, name="z_planes%d" % b) for b in range(BLOCKS)]
+        dy_planes = [keep.tile([P, PASSES, PACK, P], F32, name="dy_planes%d" % b) for b in range(LAST)]
+        g_bf = keep.tile([P, PASSES, BLOCKS, P, PACK], BF16, name="g_bf", align_bytes=64)
         g_codes = keep.tile([P, PASSES, DV], U32, name="g_codes", align_bytes=64)
         g_scales = keep.tile([P, PASSES, DV], U8, name="g_scales", align_bytes=64)
-        x_bf = keep.tile([P, X_BLOCKS, PASSES, P * PACK], BF16, name="x_bf", align_bytes=64)
-        x_codes = keep.tile([P, X_BLOCKS, PASSES, P], U32, name="x_codes", align_bytes=64)
-        x_scales = keep.tile([P, X_BLOCKS, PASSES, P], U8, name="x_scales", align_bytes=64)
-        results = [keep.tile([P, DV], F32, name="result%d" % b) for b in range(X_BLOCKS)]
-
-        def tokens(h):
-            return slice(h * K_PASS, (h + 1) * K_PASS)
-
-        def in_token_order(planes):
-            return planes.rearrange("n j (g i) -> n g j i", i=RUN)
+        x_words = [keep.tile([P, T // 2], F32, name="x_words%d" % b) for b in range(BLOCKS)]
+        x_bf = keep.tile([P, BLOCKS, T], BF16, name="x_bf", align_bytes=64)
+        x_codes = keep.tile([P, BLOCKS, PASSES, P], U32, name="x_codes", align_bytes=64)
+        x_scales = keep.tile([P, BLOCKS, PASSES, P], U8, name="x_scales", align_bytes=64)
+        results = [keep.tile([P, DV], F32, name="result%d" % b) for b in range(BLOCKS)]
 
         def gather(b, h):
-            nc.vector.tensor_copy(
-                in_token_order(picked[b][:, h].bitcast(U32)),
-                books[b][:].bitcast(U32).indirect(offsets[:, h * LIST_COLS : (h + 1) * LIST_COLS]),
-            )
-
-        def form_g(b, h):
-            for planes, raw, factor in ((z_scaled, zs, -1.0), (dy_scaled, dys, -1.0 / BETA)):
-                nc.scalar.mul(
-                    in_token_order(planes[b][:, h]),
-                    raw[b][:, tokens(h)].rearrange("n (g j i) -> n g j i", j=PACK, i=RUN),
-                    factor,
-                )
-            bank = banks.tile([P, PACK, P], F32, name="bank")
-            terms = [[planes[b][:, h, j, :] for j in range(PACK)] for planes in (picked, z_scaled, dy_scaled)]
-            for i in range(len(terms)):
-                for j in range(PACK):
-                    nc.tensor.matmul(
-                        bank[:, j, :],
-                        terms[i][j],
-                        ident[:],
-                        start=(i == 0 and j == 0),
-                        stop=(i == len(terms) - 1 and j == PACK - 1),
-                        is_transpose=True,
-                    )
             nc.vector.tensor_tensor(
-                g_bf[:, h, b],
-                bank[:].rearrange("p j n -> p n j"),
-                weights[:, h, :].unsqueeze(1).to_broadcast([P, P, PACK]),
+                picked[b][:, tokens(h)],
+                books[b][:].indirect(offsets[:, h * LIST_COLS : (h + 1) * LIST_COLS]),
+                minus_beta[:],
                 MULT,
             )
 
-        def quantize_g(b0, b1, h):
+        def form_g(b, h):
+            bank = banks.tile([P, PACK, P], F32, name="bank")
+
+            def add_planes(planes, first, last):
+                for j in range(PACK):
+                    nc.tensor.matmul(
+                        bank[:, j, :],
+                        planes[j],
+                        ident[:],
+                        start=(first and j == 0),
+                        stop=(last and j == PACK - 1),
+                        is_transpose=True,
+                    )
+
+            def into_planes(tiles):
+                return tiles[b][:, h].rearrange("n j p -> n p j")
+
+            def by_word(tiles):
+                return tiles[b][:, tokens(h)].rearrange("n (p j) -> n p j", j=PACK)
+
+            add_planes([picked[b][:, plane(h, j)] for j in range(PACK)], True, False)
+            nc.scalar.mul(into_planes(z_planes), by_word(zs), BETA)
+            add_planes([z_planes[b][:, h, j, :] for j in range(PACK)], False, False)
+            if b < LAST:
+                nc.scalar.copy(into_planes(dy_planes), by_word(dys))
+                add_planes([dy_planes[b][:, h, j, :] for j in range(PACK)], False, True)
+            else:
+                add_planes([dys[b][:, plane(h, j)] for j in range(PACK)], False, True)
+            nc.vector.tensor_tensor(g_bf[:, h, b], bank[:].rearrange("p j n -> p n j"), weights[:, h], MULT)
+
+        def quantize_g(b, h):
+            cols = slice(b * P, (b + 2) * P)
             nc.vector.quantize_mx(
-                out=g_codes[:, h, b0 * P : b1 * P].bitcast(E5M2X4),
-                scales=g_scales[:, h, b0 * P : b1 * P],
-                in_=g_bf[:, h, b0:b1].rearrange("p b n j -> p (b n j)"),
+                out=g_codes[:, h, cols].bitcast(E5M2X4),
+                scales=g_scales[:, h, cols],
+                in_=g_bf[:, h, b : b + 2].rearrange("p b n j -> p (b n j)"),
             )
 
-        def form_x(b, h0, h1, words, on_scalar):
-            pairs = words.bitcast(BF16).rearrange("m (u g i e) -> m u g i e", u=2, i=RUN, e=2)
-            raw = xs[b][:, h0 * K_PASS : h1 * K_PASS].rearrange("m (g u e i) -> m u g i e", u=2, e=2, i=RUN)
-            for u in range(2):
-                if on_scalar:
-                    nc.scalar.copy(pairs[:, u], raw[:, u])
-                else:
-                    nc.vector.tensor_copy(pairs[:, u], raw[:, u])
-            bank = x_turn.tile([P, h1 - h0, 2, P], F32, name="x_bank")
-            for h in range(h1 - h0):
+        def form_x(b, h0, h1):
+            passes = h1 - h0
+            words = x_words[b][:, h0 * 2 * P : h1 * 2 * P]
+            pairs = words.bitcast(BF16).rearrange("m (u p e) -> m p u e", u=2, e=2)
+            raw = xs[b][:, h0 * K_PASS : h1 * K_PASS].rearrange("m (p u e) -> m p u e", u=2, e=2)
+            if b < LAST:
+                nc.scalar.copy(pairs, raw)
+            else:
+                nc.vector.tensor_copy(pairs, raw)
+            bank = x_turn.tile([P, passes, 2, P], F32, name="x_bank")
+            for h in range(passes):
                 for u in range(2):
-                    first = (u * (h1 - h0) + h) * P
+                    first = (u * passes + h) * P
                     nc.tensor.transpose(bank[:, h, u, :], words[:, first : first + P], ident[:])
-            grouped = x_bf[:, b, h0:h1, :].rearrange("p h k -> p (h k)").bitcast(F32)
+            grouped = x_bf[:, b, h0 * K_PASS : h1 * K_PASS].bitcast(F32)
             nc.scalar.copy(
                 grouped.rearrange("p (h m u) -> p h m u", m=P, u=2),
                 bank[:].rearrange("p h u m -> p h m u"),
@@ -162,7 +163,7 @@ def tile_attend_gvq_s_w_kernel(tc, zT, cb, dyT, tw, xT, offs, out):
             nc.vector.quantize_mx(
                 out=x_codes[:, b, h0:h1, :].rearrange("p h m -> p (h m)").bitcast(E4M3X4),
                 scales=x_scales[:, b, h0:h1, :].rearrange("p h m -> p (h m)"),
-                in_=x_bf[:, b, h0:h1, :].rearrange("p h k -> p (h k)"),
+                in_=x_bf[:, b, h0 * K_PASS : h1 * K_PASS],
             )
 
         def multiply(acc, b, h):
@@ -176,41 +177,39 @@ def tile_attend_gvq_s_w_kernel(tc, zT, cb, dyT, tw, xT, offs, out):
                 stop=(h == PASSES - 1),
             )
 
-        x0_words = keep.tile([P, PACK * P], F32, name="x0_words")
-
-        for b in (0, 1):
-            gather(b, 0)
-            gather(b, 1)
-        form_g(0, 0)
-        form_g(0, 1)
-        gather(2, 0)
-        gather(2, 1)
-        form_g(1, 0)
-        form_g(1, 1)
-        quantize_g(0, 2, 0)
-        gather(3, 0)
-        quantize_g(0, 2, 1)
-        gather(3, 1)
-        form_g(2, 0)
-        form_g(3, 0)
-        form_x(0, 0, PASSES, x0_words[:], True)
-        quantize_x(0, 0, PASSES)
-        quantize_g(2, 4, 0)
-        form_g(2, 1)
-        form_g(3, 1)
-        for b in (1, 2):
-            form_x(b, 0, PASSES, picked[3][:, b - 1].rearrange("n j p -> n (j p)"), True)
-        quantize_x(1, 0, PASSES)
+        for b in range(2):
+            for h in range(PASSES):
+                gather(b, h)
         for h in range(PASSES):
-            form_x(3, h, h + 1, g_bf[:, 0, 2 + h].rearrange("p n j -> p (n j)").bitcast(F32), False)
-        quantize_g(2, 4, 1)
+            form_g(0, h)
+        for h in range(PASSES):
+            gather(2, h)
+        for h in range(PASSES):
+            form_g(1, h)
+        for h in range(PASSES):
+            quantize_g(0, h)
+            gather(3, h)
+        for h in range(PASSES):
+            form_g(2, h)
+        form_g(3, 0)
+        form_x(0, 0, PASSES)
+        quantize_x(0, 0, PASSES)
+        quantize_g(2, 0)
+        form_x(1, 0, PASSES)
+        form_g(3, 1)
+        quantize_x(1, 0, PASSES)
+        form_x(2, 0, PASSES)
+        for h in range(PASSES):
+            form_x(LAST, h, h + 1)
+        quantize_g(2, 1)
         quantize_x(2, 0, PASSES)
         for h in range(PASSES):
-            quantize_x(3, h, h + 1)
-        accs = [banks.tile([P, DV], F32, name="bank") for b in range(X_BLOCKS)]
-        for b in range(X_BLOCKS):
+            quantize_x(LAST, h, h + 1)
+
+        accs = [banks.tile([P, DV], F32, name="bank") for b in range(BLOCKS)]
+        for b in range(BLOCKS):
             multiply(accs[b], b, 0)
-        for b in range(X_BLOCKS):
+        for b in range(BLOCKS):
             multiply(accs[b], b, 1)
             if b % 2 == 0:
                 nc.scalar.copy(results[b][:], accs[b][:])

@@ -15,6 +15,7 @@ U8 = mybir.dt.uint8
 E4M3X4 = mybir.dt.float8_e4m3fn_x4
 E5M2X4 = mybir.dt.float8_e5m2_x4
 MULT = mybir.AluOpType.mult
+SUBTRACT = mybir.AluOpType.subtract
 
 P = 128
 PACK = 4
@@ -23,9 +24,13 @@ PASSES = T // K_PASS
 BLOCKS = DV // P
 LAST = BLOCKS - 1
 LIST_COLS = K_PASS // 16
-WINDOW = C + 16
+WINDOW = 2 * C
 X_BANKS = 2
 G_BANKS = 8 - X_BANKS
+
+
+UNITS = [(0, 0), (0, 1), (1, 0), (1, 1), (2, 0), (3, 0), (2, 1), (3, 1)]
+LAID_OUT = 5
 
 
 def tile_attend_gvq_s_w_kernel(tc, zT, cb, dyT, tw, xT, offs, out):
@@ -35,180 +40,181 @@ def tile_attend_gvq_s_w_kernel(tc, zT, cb, dyT, tw, xT, offs, out):
         banks = ctx.enter_context(tc.psum_pool(name="banks", bufs=G_BANKS))
         x_turn = ctx.enter_context(tc.psum_pool(name="x_turn", bufs=X_BANKS))
 
+        def unit_tiles(name, shape, dtype=F32):
+            return {(b, h): keep.tile(shape, dtype, name="%s%d%d" % (name, b, h)) for b, h in UNITS}
+
         offsets = keep.tile([P, T // 16], U16, name="offsets")
         books = [keep.tile([P, WINDOW], F32, name="book%d" % b) for b in range(BLOCKS)]
-        zs = [keep.tile([P, T], F32, name="z%d" % b) for b in range(BLOCKS)]
-        dys = [keep.tile([P, T], F32, name="dy%d" % b) for b in range(BLOCKS)]
-        xs = [keep.tile([P, T], F32, name="x%d" % b) for b in range(BLOCKS)]
+        zs = unit_tiles("z", [P, K_PASS])
+        dys = unit_tiles("dy", [P, K_PASS])
+        xs = unit_tiles("x", [P, K_PASS])
         tw_words = keep.tile([P, PASSES, PACK], F32, name="tw_words")
 
         def rows(b):
             return slice(b * P, (b + 1) * P)
 
-        def tokens(h):
-            return slice(h * K_PASS, (h + 1) * K_PASS)
-
-        def plane(h, j):
-            return slice(h * K_PASS + j, (h + 1) * K_PASS, PACK)
-
-        def load_book(b):
-            nc.sync.dma_start(books[b][:, :C], cb[rows(b), :])
+        def load(tiles, source, unit):
+            b, h = unit
+            nc.sync.dma_start(tiles[unit][:], source[rows(b), h * K_PASS : (h + 1) * K_PASS])
 
         nc.sync.dma_start(offsets[:], offs)
-        load_book(0)
-        load_book(1)
-        nc.sync.dma_start(tw_words[:], tw[0, :].rearrange("(h p j) -> p h j", h=PASSES, j=PACK))
+        for step, (b, h) in enumerate(UNITS):
+            if h == 0:
+                nc.sync.dma_start(books[b][:, :C], cb[rows(b), :])
+            load(zs, zT, (b, h))
+            if step == 0:
+                nc.sync.dma_start(tw_words[:], tw[0, :].rearrange("(h p j) -> p h j", h=PASSES, j=PACK))
+            load(dys, dyT, (b, h))
+            if step >= BLOCKS:
+                load(xs, xT, (step - BLOCKS, 0))
         for b in range(BLOCKS):
-            nc.sync.dma_start(zs[b][:], zT[rows(b), :])
-            nc.sync.dma_start(dys[b][:], dyT[rows(b), :])
-            if b + 2 < BLOCKS:
-                load_book(b + 2)
-            if b >= 1:
-                nc.sync.dma_start(xs[b - 1][:], xT[rows(b - 1), :])
-        for h in range(PASSES):
-            nc.sync.dma_start(xs[LAST][:, tokens(h)], xT[rows(LAST), tokens(h)])
+            load(xs, xT, (b, 1))
 
-        ones = keep.tile([P, K_PASS], F32, name="ones")
-        minus_beta = keep.tile([P, K_PASS], F32, name="minus_beta")
-        nc.gpsimd.memset(ones[:], 1.0)
-        nc.scalar.mul(minus_beta[:], ones[:], -BETA)
         for b in range(BLOCKS):
-            nc.gpsimd.memset(books[b][:, C:], 0.0)
+            nc.vector.memset(books[b][:, C:], 0.0)
         ident = keep.tile([P, P], F32, name="ident")
         make_identity(nc, ident[:])
 
         weights = keep.tile([P, PASSES, P, PACK], F32, name="weights")
-        for h in range(PASSES):
-            nc.scalar.copy(weights[:, h], tw_words[:, h, :].unsqueeze(1).to_broadcast([P, P, PACK]))
 
-        picked = [keep.tile([P, T], F32, name="picked%d" % b) for b in range(BLOCKS)]
-        z_planes = [keep.tile([P, PASSES, PACK, P], F32, name="z_planes%d" % b) for b in range(BLOCKS)]
-        dy_planes = [keep.tile([P, PASSES, PACK, P], F32, name="dy_planes%d" % b) for b in range(LAST)]
+        def spread_weights(h):
+            nc.scalar.mul(weights[:, h], tw_words[:, h, :].unsqueeze(1).to_broadcast([P, P, PACK]), -BETA)
+
+        gaps = unit_tiles("gap", [P, K_PASS])
+        gap_planes = {unit: keep.tile([P, PACK, P], F32, name="gap_planes%d%d" % unit) for unit in UNITS[:LAID_OUT]}
+        dy_planes = unit_tiles("dy_planes", [P, PACK, P])
         g_bf = keep.tile([P, PASSES, BLOCKS, P, PACK], BF16, name="g_bf", align_bytes=64)
         g_codes = keep.tile([P, PASSES, DV], U32, name="g_codes", align_bytes=64)
         g_scales = keep.tile([P, PASSES, DV], U8, name="g_scales", align_bytes=64)
-        x_words = [keep.tile([P, T // 2], F32, name="x_words%d" % b) for b in range(BLOCKS)]
-        x_bf = keep.tile([P, BLOCKS, T], BF16, name="x_bf", align_bytes=64)
-        x_codes = keep.tile([P, BLOCKS, PASSES, P], U32, name="x_codes", align_bytes=64)
-        x_scales = keep.tile([P, BLOCKS, PASSES, P], U8, name="x_scales", align_bytes=64)
+        x_words = unit_tiles("x_words", [P, 2, P])
+        x_bf = keep.tile([P, PASSES, BLOCKS, P, PACK], BF16, name="x_bf", align_bytes=64)
+        x_codes = keep.tile([P, PASSES, D], U32, name="x_codes", align_bytes=64)
+        x_scales = keep.tile([P, PASSES, D], U8, name="x_scales", align_bytes=64)
         results = [keep.tile([P, DV], F32, name="result%d" % b) for b in range(BLOCKS)]
+        sums = {}
 
-        def gather(b, h):
+        def gather(unit):
+            b, h = unit
             nc.vector.tensor_tensor(
-                picked[b][:, tokens(h)],
+                gaps[unit][:],
                 books[b][:].indirect(offsets[:, h * LIST_COLS : (h + 1) * LIST_COLS]),
-                minus_beta[:],
-                MULT,
+                zs[unit][:],
+                SUBTRACT,
             )
 
-        def form_g(b, h):
+        def turn_g(unit):
             bank = banks.tile([P, PACK, P], F32, name="bank")
-
-            def add_planes(planes, first, last):
-                for j in range(PACK):
-                    nc.tensor.matmul(
-                        bank[:, j, :],
-                        planes[j],
-                        ident[:],
-                        start=(first and j == 0),
-                        stop=(last and j == PACK - 1),
-                        is_transpose=True,
-                    )
-
-            def into_planes(tiles):
-                return tiles[b][:, h].rearrange("n j p -> n p j")
-
-            def by_word(tiles):
-                return tiles[b][:, tokens(h)].rearrange("n (p j) -> n p j", j=PACK)
-
-            add_planes([picked[b][:, plane(h, j)] for j in range(PACK)], True, False)
-            nc.scalar.mul(into_planes(z_planes), by_word(zs), BETA)
-            add_planes([z_planes[b][:, h, j, :] for j in range(PACK)], False, False)
-            if b < LAST:
-                nc.scalar.copy(into_planes(dy_planes), by_word(dys))
-                add_planes([dy_planes[b][:, h, j, :] for j in range(PACK)], False, True)
+            sums[unit] = bank
+            nc.scalar.mul(
+                dy_planes[unit][:].rearrange("n j p -> n p j"),
+                dys[unit][:].rearrange("n (p j) -> n p j", j=PACK),
+                -1.0 / BETA,
+            )
+            for j in range(PACK):
+                nc.tensor.matmul(
+                    bank[:, j, :], dy_planes[unit][:, j, :], ident[:], start=(j == 0), stop=False, is_transpose=True
+                )
+            if unit in gap_planes:
+                nc.scalar.copy(
+                    gap_planes[unit][:].rearrange("n j p -> n p j"),
+                    gaps[unit][:].rearrange("n (p j) -> n p j", j=PACK),
+                )
+                planes = [gap_planes[unit][:, j, :] for j in range(PACK)]
             else:
-                add_planes([dys[b][:, plane(h, j)] for j in range(PACK)], False, True)
-            nc.vector.tensor_tensor(g_bf[:, h, b], bank[:].rearrange("p j n -> p n j"), weights[:, h], MULT)
+                planes = [gaps[unit][:, j::PACK] for j in range(PACK)]
+            for j in range(PACK):
+                nc.tensor.matmul(
+                    bank[:, j, :], planes[j], ident[:], start=False, stop=(j == PACK - 1), is_transpose=True
+                )
 
-        def quantize_g(b, h):
-            cols = slice(b * P, (b + 2) * P)
+        def weigh(unit):
+            b, h = unit
+            nc.vector.tensor_tensor(g_bf[:, h, b], sums[unit][:].rearrange("p j n -> p n j"), weights[:, h], MULT)
+
+        def quantize(codes, scales, values, dtype, h, b0, b1):
+            cols = slice(b0 * P, b1 * P)
             nc.vector.quantize_mx(
-                out=g_codes[:, h, cols].bitcast(E5M2X4),
-                scales=g_scales[:, h, cols],
-                in_=g_bf[:, h, b : b + 2].rearrange("p b n j -> p (b n j)"),
+                out=codes[:, h, cols].bitcast(dtype),
+                scales=scales[:, h, cols],
+                in_=values[:, h, b0:b1].rearrange("p b n j -> p (b n j)"),
             )
 
-        def form_x(b, h0, h1):
-            passes = h1 - h0
-            words = x_words[b][:, h0 * 2 * P : h1 * 2 * P]
-            pairs = words.bitcast(BF16).rearrange("m (u p e) -> m p u e", u=2, e=2)
-            raw = xs[b][:, h0 * K_PASS : h1 * K_PASS].rearrange("m (p u e) -> m p u e", u=2, e=2)
-            if b < LAST:
-                nc.scalar.copy(pairs, raw)
-            else:
-                nc.vector.tensor_copy(pairs, raw)
-            bank = x_turn.tile([P, passes, 2, P], F32, name="x_bank")
-            for h in range(passes):
+        def quantize_g(h, b0, b1):
+            quantize(g_codes, g_scales, g_bf, E5M2X4, h, b0, b1)
+
+        def quantize_x(h, b0, b1):
+            quantize(x_codes, x_scales, x_bf, E4M3X4, h, b0, b1)
+
+        def form_x(h, b0, b1):
+            bank = x_turn.tile([P, b1 - b0, 2, P], F32, name="x_bank")
+            for b in range(b0, b1):
+                words = x_words[b, h]
+                nc.scalar.copy(
+                    words[:].rearrange("m u p -> m (u p)").bitcast(BF16).rearrange("m (u p e) -> m p u e", u=2, e=2),
+                    xs[b, h][:].rearrange("m (p u e) -> m p u e", u=2, e=2),
+                )
                 for u in range(2):
-                    first = (u * passes + h) * P
-                    nc.tensor.transpose(bank[:, h, u, :], words[:, first : first + P], ident[:])
-            grouped = x_bf[:, b, h0 * K_PASS : h1 * K_PASS].bitcast(F32)
+                    nc.tensor.transpose(bank[:, b - b0, u, :], words[:, u, :], ident[:])
+            grouped = x_bf[:, h, b0:b1].rearrange("p b m j -> p (b m j)").bitcast(F32)
             nc.scalar.copy(
-                grouped.rearrange("p (h m u) -> p h m u", m=P, u=2),
-                bank[:].rearrange("p h u m -> p h m u"),
-            )
-
-        def quantize_x(b, h0, h1):
-            nc.vector.quantize_mx(
-                out=x_codes[:, b, h0:h1, :].rearrange("p h m -> p (h m)").bitcast(E4M3X4),
-                scales=x_scales[:, b, h0:h1, :].rearrange("p h m -> p (h m)"),
-                in_=x_bf[:, b, h0 * K_PASS : h1 * K_PASS],
+                grouped.rearrange("p (b m u) -> p b m u", m=P, u=2),
+                bank[:].rearrange("p b u m -> p b m u"),
             )
 
         def multiply(acc, b, h):
             nc.tensor.matmul_mx(
                 out=acc[:],
-                lhsT=x_codes[:, b, h, :].bitcast(E4M3X4),
-                lhsT_scale=x_scales[:, b, h, :],
+                lhsT=x_codes[:, h, rows(b)].bitcast(E4M3X4),
+                lhsT_scale=x_scales[:, h, rows(b)],
                 rhs=g_codes[:, h, :].bitcast(E5M2X4),
                 rhs_scale=g_scales[:, h, :],
                 start=(h == 0),
                 stop=(h == PASSES - 1),
             )
 
-        for b in range(2):
-            for h in range(PASSES):
-                gather(b, h)
-        for h in range(PASSES):
-            form_g(0, h)
-        for h in range(PASSES):
-            gather(2, h)
-        for h in range(PASSES):
-            form_g(1, h)
-        for h in range(PASSES):
-            quantize_g(0, h)
-            gather(3, h)
-        for h in range(PASSES):
-            form_g(2, h)
-        form_g(3, 0)
-        form_x(0, 0, PASSES)
-        quantize_x(0, 0, PASSES)
-        quantize_g(2, 0)
-        form_x(1, 0, PASSES)
-        form_g(3, 1)
-        quantize_x(1, 0, PASSES)
-        form_x(2, 0, PASSES)
-        for h in range(PASSES):
-            form_x(LAST, h, h + 1)
-        quantize_g(2, 1)
-        quantize_x(2, 0, PASSES)
-        for h in range(PASSES):
-            quantize_x(LAST, h, h + 1)
-
+        spread_weights(0)
+        for unit in UNITS[:3]:
+            gather(unit)
+        turn_g(UNITS[0])
+        spread_weights(1)
+        weigh(UNITS[0])
+        gather(UNITS[3])
+        turn_g(UNITS[1])
+        weigh(UNITS[1])
+        gather(UNITS[4])
+        turn_g(UNITS[2])
+        weigh(UNITS[2])
+        gather(UNITS[5])
+        quantize_g(0, 0, 2)
+        turn_g(UNITS[3])
+        weigh(UNITS[3])
+        form_x(0, 0, 2)
+        gather(UNITS[6])
+        quantize_g(1, 0, 2)
+        turn_g(UNITS[4])
+        weigh(UNITS[4])
+        quantize_x(0, 0, 2)
+        turn_g(UNITS[5])
+        weigh(UNITS[5])
+        form_x(0, 2, 4)
+        quantize_x(0, 2, 4)
+        gather(UNITS[7])
+        quantize_g(0, 2, 4)
+        turn_g(UNITS[6])
+        turn_g(UNITS[7])
         accs = [banks.tile([P, DV], F32, name="bank") for b in range(BLOCKS)]
         for b in range(BLOCKS):
             multiply(accs[b], b, 0)
+        weigh(UNITS[6])
+        form_x(1, 0, 2)
+        quantize_g(1, 2, 3)
+        quantize_x(1, 0, 2)
+        weigh(UNITS[7])
+        form_x(1, 2, 3)
+        form_x(1, 3, 4)
+        quantize_x(1, 2, 3)
+        quantize_g(1, 3, 4)
+        quantize_x(1, 3, 4)
         for b in range(BLOCKS):
             multiply(accs[b], b, 1)
             if b % 2 == 0:

@@ -30,7 +30,9 @@ G_BANKS = 8 - X_BANKS
 
 
 UNITS = [(0, 0), (0, 1), (1, 0), (1, 1), (2, 0), (3, 0), (2, 1), (3, 1)]
-LAID_OUT = 5
+GATHERS = [(0, 0), (1, 0), (0, 1), (1, 1), (2, 0), (2, 1), (3, 0), (3, 1)]
+EARLY = GATHERS[:2]
+LAID_OUT = 4
 
 
 def tile_attend_gvq_s_w_kernel(tc, zT, cb, dyT, tw, xT, offs, out):
@@ -45,30 +47,39 @@ def tile_attend_gvq_s_w_kernel(tc, zT, cb, dyT, tw, xT, offs, out):
 
         offsets = keep.tile([P, T // 16], U16, name="offsets")
         books = [keep.tile([P, WINDOW], F32, name="book%d" % b) for b in range(BLOCKS)]
-        zs = unit_tiles("z", [P, K_PASS])
-        dys = unit_tiles("dy", [P, K_PASS])
-        xs = unit_tiles("x", [P, K_PASS])
+        zs = [keep.tile([P, T], F32, name="z%d" % b) for b in range(BLOCKS)]
+        dys = [keep.tile([P, T], F32, name="dy%d" % b) for b in range(BLOCKS)]
+        xs = [keep.tile([P, T], F32, name="x%d" % b) for b in range(BLOCKS)]
         tw_words = keep.tile([P, PASSES, PACK], F32, name="tw_words")
 
         def rows(b):
             return slice(b * P, (b + 1) * P)
 
-        def load(tiles, source, unit):
-            b, h = unit
-            nc.sync.dma_start(tiles[unit][:], source[rows(b), h * K_PASS : (h + 1) * K_PASS])
+        def tokens(h):
+            return slice(h * K_PASS, (h + 1) * K_PASS)
 
+        def load(tiles, source, b):
+            nc.sync.dma_start(tiles[b][:, : source.shape[1]], source[rows(b), :])
+
+        load(books, cb, 0)
         nc.sync.dma_start(offsets[:], offs)
-        for step, (b, h) in enumerate(UNITS):
-            if h == 0:
-                nc.sync.dma_start(books[b][:, :C], cb[rows(b), :])
-            load(zs, zT, (b, h))
-            if step == 0:
-                nc.sync.dma_start(tw_words[:], tw[0, :].rearrange("(h p j) -> p h j", h=PASSES, j=PACK))
-            load(dys, dyT, (b, h))
-            if step >= BLOCKS:
-                load(xs, xT, (step - BLOCKS, 0))
-        for b in range(BLOCKS):
-            load(xs, xT, (b, 1))
+        load(books, cb, 1)
+        nc.sync.dma_start(tw_words[:], tw[0, :].rearrange("(h p j) -> p h j", h=PASSES, j=PACK))
+        load(zs, zT, 0)
+        load(zs, zT, 1)
+        load(books, cb, 2)
+        load(zs, zT, 2)
+        load(dys, dyT, 0)
+        load(books, cb, 3)
+        load(zs, zT, 3)
+        load(dys, dyT, 1)
+        load(xs, xT, 0)
+        load(dys, dyT, 2)
+        load(dys, dyT, 3)
+        load(xs, xT, 1)
+        load(xs, xT, 2)
+        for h in range(PASSES):
+            nc.sync.dma_start(xs[LAST][:, tokens(h)], xT[rows(LAST), tokens(h)])
 
         for b in range(BLOCKS):
             nc.vector.memset(books[b][:, C:], 0.0)
@@ -81,140 +92,146 @@ def tile_attend_gvq_s_w_kernel(tc, zT, cb, dyT, tw, xT, offs, out):
             nc.scalar.mul(weights[:, h], tw_words[:, h, :].unsqueeze(1).to_broadcast([P, P, PACK]), -BETA)
 
         gaps = unit_tiles("gap", [P, K_PASS])
-        gap_planes = {unit: keep.tile([P, PACK, P], F32, name="gap_planes%d%d" % unit) for unit in UNITS[:LAID_OUT]}
+        gap_planes = {unit: keep.tile([P, PACK, P], F32, name="gap_planes%d%d" % unit) for unit in GATHERS[:LAID_OUT]}
+        z_planes = {unit: keep.tile([P, PACK, P], F32, name="z_planes%d%d" % unit) for unit in EARLY}
         dy_planes = unit_tiles("dy_planes", [P, PACK, P])
         g_bf = keep.tile([P, PASSES, BLOCKS, P, PACK], BF16, name="g_bf", align_bytes=64)
         g_codes = keep.tile([P, PASSES, DV], U32, name="g_codes", align_bytes=64)
         g_scales = keep.tile([P, PASSES, DV], U8, name="g_scales", align_bytes=64)
-        x_words = unit_tiles("x_words", [P, 2, P])
-        x_bf = keep.tile([P, PASSES, BLOCKS, P, PACK], BF16, name="x_bf", align_bytes=64)
-        x_codes = keep.tile([P, PASSES, D], U32, name="x_codes", align_bytes=64)
-        x_scales = keep.tile([P, PASSES, D], U8, name="x_scales", align_bytes=64)
+        x_words = [keep.tile([P, T // 2], F32, name="x_words%d" % b) for b in range(BLOCKS)]
+        x_bf = keep.tile([P, BLOCKS, T], BF16, name="x_bf", align_bytes=64)
+        x_codes = keep.tile([P, BLOCKS, PASSES, P], U32, name="x_codes", align_bytes=64)
+        x_scales = keep.tile([P, BLOCKS, PASSES, P], U8, name="x_scales", align_bytes=64)
         results = [keep.tile([P, DV], F32, name="result%d" % b) for b in range(BLOCKS)]
         sums = {}
 
         def gather(unit):
             b, h = unit
-            nc.vector.tensor_tensor(
-                gaps[unit][:],
-                books[b][:].indirect(offsets[:, h * LIST_COLS : (h + 1) * LIST_COLS]),
-                zs[unit][:],
-                SUBTRACT,
-            )
+            picked = books[b][:].indirect(offsets[:, h * LIST_COLS : (h + 1) * LIST_COLS])
+            if unit in EARLY:
+                nc.vector.tensor_copy(gaps[unit][:], picked)
+            else:
+                nc.vector.tensor_tensor(gaps[unit][:], picked, zs[b][:, tokens(h)], SUBTRACT)
 
-        def turn_g(unit):
+        def lay_out(planes, values, factor):
+            nc.scalar.mul(planes[:].rearrange("n j p -> n p j"), values.rearrange("n (p j) -> n p j", j=PACK), factor)
+            return [planes[:, j, :] for j in range(PACK)]
+
+        def add_planes(bank, planes, first, last):
+            for j in range(PACK):
+                nc.tensor.matmul(
+                    bank[:, j, :],
+                    planes[j],
+                    ident[:],
+                    start=(first and j == 0),
+                    stop=(last and j == PACK - 1),
+                    is_transpose=True,
+                )
+
+        def turn_gap(unit):
+            b, h = unit
             bank = banks.tile([P, PACK, P], F32, name="bank")
             sums[unit] = bank
-            nc.scalar.mul(
-                dy_planes[unit][:].rearrange("n j p -> n p j"),
-                dys[unit][:].rearrange("n (p j) -> n p j", j=PACK),
-                -1.0 / BETA,
-            )
-            for j in range(PACK):
-                nc.tensor.matmul(
-                    bank[:, j, :], dy_planes[unit][:, j, :], ident[:], start=(j == 0), stop=False, is_transpose=True
-                )
             if unit in gap_planes:
-                nc.scalar.copy(
-                    gap_planes[unit][:].rearrange("n j p -> n p j"),
-                    gaps[unit][:].rearrange("n (p j) -> n p j", j=PACK),
-                )
-                planes = [gap_planes[unit][:, j, :] for j in range(PACK)]
+                add_planes(bank, lay_out(gap_planes[unit], gaps[unit][:], 1.0), True, False)
             else:
-                planes = [gaps[unit][:, j::PACK] for j in range(PACK)]
-            for j in range(PACK):
-                nc.tensor.matmul(
-                    bank[:, j, :], planes[j], ident[:], start=False, stop=(j == PACK - 1), is_transpose=True
-                )
+                add_planes(bank, [gaps[unit][:, j::PACK] for j in range(PACK)], True, False)
+            if unit in EARLY:
+                add_planes(bank, lay_out(z_planes[unit], zs[b][:, tokens(h)], -1.0), False, False)
+
+        def turn_dy(unit):
+            b, h = unit
+            add_planes(sums[unit], lay_out(dy_planes[unit], dys[b][:, tokens(h)], -1.0 / BETA), False, True)
 
         def weigh(unit):
             b, h = unit
             nc.vector.tensor_tensor(g_bf[:, h, b], sums[unit][:].rearrange("p j n -> p n j"), weights[:, h], MULT)
 
-        def quantize(codes, scales, values, dtype, h, b0, b1):
+        def quantize_g(h, b0, b1):
             cols = slice(b0 * P, b1 * P)
             nc.vector.quantize_mx(
-                out=codes[:, h, cols].bitcast(dtype),
-                scales=scales[:, h, cols],
-                in_=values[:, h, b0:b1].rearrange("p b n j -> p (b n j)"),
+                out=g_codes[:, h, cols].bitcast(E5M2X4),
+                scales=g_scales[:, h, cols],
+                in_=g_bf[:, h, b0:b1].rearrange("p b n j -> p (b n j)"),
             )
 
-        def quantize_g(h, b0, b1):
-            quantize(g_codes, g_scales, g_bf, E5M2X4, h, b0, b1)
-
-        def quantize_x(h, b0, b1):
-            quantize(x_codes, x_scales, x_bf, E4M3X4, h, b0, b1)
-
-        def form_x(h, b0, b1):
-            bank = x_turn.tile([P, b1 - b0, 2, P], F32, name="x_bank")
-            for b in range(b0, b1):
-                words = x_words[b, h]
-                nc.scalar.copy(
-                    words[:].rearrange("m u p -> m (u p)").bitcast(BF16).rearrange("m (u p e) -> m p u e", u=2, e=2),
-                    xs[b, h][:].rearrange("m (p u e) -> m p u e", u=2, e=2),
-                )
+        def form_x(b, h0, h1):
+            passes = h1 - h0
+            words = x_words[b][:, h0 * 2 * P : h1 * 2 * P]
+            pairs = words.bitcast(BF16).rearrange("m (u p e) -> m p u e", u=2, e=2)
+            raw = xs[b][:, h0 * K_PASS : h1 * K_PASS].rearrange("m (p u e) -> m p u e", u=2, e=2)
+            if b < LAST:
+                nc.scalar.copy(pairs, raw)
+            else:
+                nc.vector.tensor_copy(pairs, raw)
+            bank = x_turn.tile([P, passes, 2, P], F32, name="x_bank")
+            for h in range(passes):
                 for u in range(2):
-                    nc.tensor.transpose(bank[:, b - b0, u, :], words[:, u, :], ident[:])
-            grouped = x_bf[:, h, b0:b1].rearrange("p b m j -> p (b m j)").bitcast(F32)
+                    first = (u * passes + h) * P
+                    nc.tensor.transpose(bank[:, h, u, :], words[:, first : first + P], ident[:])
+            grouped = x_bf[:, b, h0 * K_PASS : h1 * K_PASS].bitcast(F32)
             nc.scalar.copy(
-                grouped.rearrange("p (b m u) -> p b m u", m=P, u=2),
-                bank[:].rearrange("p b u m -> p b m u"),
+                grouped.rearrange("p (h m u) -> p h m u", m=P, u=2),
+                bank[:].rearrange("p h u m -> p h m u"),
+            )
+
+        def quantize_x(b, h0, h1):
+            nc.vector.quantize_mx(
+                out=x_codes[:, b, h0:h1, :].rearrange("p h m -> p (h m)").bitcast(E4M3X4),
+                scales=x_scales[:, b, h0:h1, :].rearrange("p h m -> p (h m)"),
+                in_=x_bf[:, b, h0 * K_PASS : h1 * K_PASS],
             )
 
         def multiply(acc, b, h):
             nc.tensor.matmul_mx(
                 out=acc[:],
-                lhsT=x_codes[:, h, rows(b)].bitcast(E4M3X4),
-                lhsT_scale=x_scales[:, h, rows(b)],
+                lhsT=x_codes[:, b, h, :].bitcast(E4M3X4),
+                lhsT_scale=x_scales[:, b, h, :],
                 rhs=g_codes[:, h, :].bitcast(E5M2X4),
                 rhs_scale=g_scales[:, h, :],
                 start=(h == 0),
                 stop=(h == PASSES - 1),
             )
 
-        spread_weights(0)
-        for unit in UNITS[:3]:
+        for h in range(PASSES):
+            spread_weights(h)
+        for unit in GATHERS[:6]:
             gather(unit)
-        turn_g(UNITS[0])
-        spread_weights(1)
-        weigh(UNITS[0])
-        gather(UNITS[3])
-        turn_g(UNITS[1])
-        weigh(UNITS[1])
-        gather(UNITS[4])
-        turn_g(UNITS[2])
-        weigh(UNITS[2])
-        gather(UNITS[5])
-        quantize_g(0, 0, 2)
-        turn_g(UNITS[3])
-        weigh(UNITS[3])
-        form_x(0, 0, 2)
-        gather(UNITS[6])
-        quantize_g(1, 0, 2)
-        turn_g(UNITS[4])
-        weigh(UNITS[4])
-        quantize_x(0, 0, 2)
-        turn_g(UNITS[5])
-        weigh(UNITS[5])
-        form_x(0, 2, 4)
-        quantize_x(0, 2, 4)
-        gather(UNITS[7])
+            turn_gap(unit)
+        for unit in UNITS[:2]:
+            turn_dy(unit)
+            weigh(unit)
+        for unit in GATHERS[6:]:
+            gather(unit)
+        for unit in UNITS[2:4]:
+            turn_dy(unit)
+        for unit in GATHERS[6:]:
+            turn_gap(unit)
+        for unit in UNITS[2:4]:
+            weigh(unit)
+        for h in range(PASSES):
+            quantize_g(h, 0, 2)
+        form_x(0, 0, PASSES)
+        for unit in UNITS[4:6]:
+            turn_dy(unit)
+            weigh(unit)
+        quantize_x(0, 0, PASSES)
         quantize_g(0, 2, 4)
-        turn_g(UNITS[6])
-        turn_g(UNITS[7])
+        for unit in UNITS[6:]:
+            turn_dy(unit)
+            weigh(unit)
+        form_x(1, 0, PASSES)
+        quantize_x(1, 0, PASSES)
+        quantize_g(1, 2, 4)
+        form_x(2, 0, PASSES)
+        for h in range(PASSES):
+            form_x(LAST, h, h + 1)
+        quantize_x(2, 0, PASSES)
+        for h in range(PASSES):
+            quantize_x(LAST, h, h + 1)
         accs = [banks.tile([P, DV], F32, name="bank") for b in range(BLOCKS)]
         for b in range(BLOCKS):
             multiply(accs[b], b, 0)
-        weigh(UNITS[6])
-        form_x(1, 0, 2)
-        quantize_g(1, 2, 3)
-        quantize_x(1, 0, 2)
-        weigh(UNITS[7])
-        form_x(1, 2, 3)
-        form_x(1, 3, 4)
-        quantize_x(1, 2, 3)
-        quantize_g(1, 3, 4)
-        quantize_x(1, 3, 4)
         for b in range(BLOCKS):
             multiply(accs[b], b, 1)
             if b % 2 == 0:

@@ -31,6 +31,7 @@ G_BANKS = 8 - X_BANKS
 
 UNITS = [(0, 0), (0, 1), (1, 0), (1, 1), (2, 0), (3, 0), (2, 1), (3, 1)]
 GATHERS = [(0, 0), (1, 0), (0, 1), (1, 1), (2, 0), (2, 1), (3, 0), (3, 1)]
+BANK = {(0, 0): 0, (1, 0): 1, (0, 1): 2, (1, 1): 3, (2, 0): 4, (2, 1): 0, (3, 0): 2, (3, 1): 1}
 EARLY = GATHERS[:2]
 LAID_OUT = 4
 
@@ -39,7 +40,7 @@ def tile_attend_gvq_s_w_kernel(tc, zT, cb, dyT, tw, xT, offs, out):
     nc = tc.nc
     with ExitStack() as ctx:
         keep = ctx.enter_context(tc.tile_pool(name="keep", bufs=1))
-        banks = ctx.enter_context(tc.psum_pool(name="banks", bufs=G_BANKS))
+        banks = ctx.enter_context(tc.psum_pool(name="banks", bufs=1))
         x_turn = ctx.enter_context(tc.psum_pool(name="x_turn", bufs=X_BANKS))
 
         def unit_tiles(name, shape, dtype=F32):
@@ -63,18 +64,18 @@ def tile_attend_gvq_s_w_kernel(tc, zT, cb, dyT, tw, xT, offs, out):
 
         load(books, cb, 0)
         nc.sync.dma_start(offsets[:], offs)
-        load(books, cb, 1)
         nc.sync.dma_start(tw_words[:], tw[0, :].rearrange("(h p j) -> p h j", h=PASSES, j=PACK))
+        load(books, cb, 1)
         load(zs, zT, 0)
         load(zs, zT, 1)
         load(books, cb, 2)
         load(zs, zT, 2)
         load(dys, dyT, 0)
         load(books, cb, 3)
-        load(zs, zT, 3)
         load(dys, dyT, 1)
-        load(xs, xT, 0)
+        load(zs, zT, 3)
         load(dys, dyT, 2)
+        load(xs, xT, 0)
         load(dys, dyT, 3)
         load(xs, xT, 1)
         load(xs, xT, 2)
@@ -91,10 +92,12 @@ def tile_attend_gvq_s_w_kernel(tc, zT, cb, dyT, tw, xT, offs, out):
         def spread_weights(h):
             nc.scalar.mul(weights[:, h], tw_words[:, h, :].unsqueeze(1).to_broadcast([P, P, PACK]), -BETA)
 
-        gaps = unit_tiles("gap", [P, K_PASS])
         gap_planes = {unit: keep.tile([P, PACK, P], F32, name="gap_planes%d%d" % unit) for unit in GATHERS[:LAID_OUT]}
         z_planes = {unit: keep.tile([P, PACK, P], F32, name="z_planes%d%d" % unit) for unit in EARLY}
         dy_planes = unit_tiles("dy_planes", [P, PACK, P])
+        gaps = {unit: keep.tile([P, K_PASS], F32, name="gap%d%d" % unit)[:] for unit in GATHERS[:6]}
+        gaps[3, 0] = dy_planes[0, 1][:].rearrange("n j p -> n (j p)")
+        gaps[3, 1] = dy_planes[1, 0][:].rearrange("n j p -> n (j p)")
         g_bf = keep.tile([P, PASSES, BLOCKS, P, PACK], BF16, name="g_bf", align_bytes=64)
         g_codes = keep.tile([P, PASSES, DV], U32, name="g_codes", align_bytes=64)
         g_scales = keep.tile([P, PASSES, DV], U8, name="g_scales", align_bytes=64)
@@ -109,9 +112,9 @@ def tile_attend_gvq_s_w_kernel(tc, zT, cb, dyT, tw, xT, offs, out):
             b, h = unit
             picked = books[b][:].indirect(offsets[:, h * LIST_COLS : (h + 1) * LIST_COLS])
             if unit in EARLY:
-                nc.vector.tensor_copy(gaps[unit][:], picked)
+                nc.vector.tensor_copy(gaps[unit], picked)
             else:
-                nc.vector.tensor_tensor(gaps[unit][:], picked, zs[b][:, tokens(h)], SUBTRACT)
+                nc.vector.tensor_tensor(gaps[unit], picked, zs[b][:, tokens(h)], SUBTRACT)
 
         def lay_out(planes, values, factor):
             nc.scalar.mul(planes[:].rearrange("n j p -> n p j"), values.rearrange("n (p j) -> n p j", j=PACK), factor)
@@ -128,20 +131,26 @@ def tile_attend_gvq_s_w_kernel(tc, zT, cb, dyT, tw, xT, offs, out):
                     is_transpose=True,
                 )
 
+        def bank_of(unit):
+            first = unit not in sums
+            if first:
+                sums[unit] = banks.tile([P, PACK, P], F32, name="bank%d" % BANK[unit])
+            return sums[unit], first
+
         def turn_gap(unit):
             b, h = unit
-            bank = banks.tile([P, PACK, P], F32, name="bank")
-            sums[unit] = bank
+            bank, first = bank_of(unit)
             if unit in gap_planes:
-                add_planes(bank, lay_out(gap_planes[unit], gaps[unit][:], 1.0), True, False)
+                add_planes(bank, lay_out(gap_planes[unit], gaps[unit], 1.0), first, not first)
             else:
-                add_planes(bank, [gaps[unit][:, j::PACK] for j in range(PACK)], True, False)
+                add_planes(bank, [gaps[unit][:, j::PACK] for j in range(PACK)], first, not first)
             if unit in EARLY:
                 add_planes(bank, lay_out(z_planes[unit], zs[b][:, tokens(h)], -1.0), False, False)
 
         def turn_dy(unit):
             b, h = unit
-            add_planes(sums[unit], lay_out(dy_planes[unit], dys[b][:, tokens(h)], -1.0 / BETA), False, True)
+            bank, first = bank_of(unit)
+            add_planes(bank, lay_out(dy_planes[unit], dys[b][:, tokens(h)], -1.0 / BETA), first, not first)
 
         def weigh(unit):
             b, h = unit
@@ -195,30 +204,34 @@ def tile_attend_gvq_s_w_kernel(tc, zT, cb, dyT, tw, xT, offs, out):
 
         for h in range(PASSES):
             spread_weights(h)
-        for unit in GATHERS[:6]:
+        for unit in GATHERS[:5]:
             gather(unit)
             turn_gap(unit)
+        gather(GATHERS[5])
         for unit in UNITS[:2]:
             turn_dy(unit)
             weigh(unit)
-        for unit in GATHERS[6:]:
-            gather(unit)
+        turn_gap(GATHERS[5])
         for unit in UNITS[2:4]:
             turn_dy(unit)
-        for unit in GATHERS[6:]:
-            turn_gap(unit)
-        for unit in UNITS[2:4]:
-            weigh(unit)
+        gather(GATHERS[6])
+        turn_gap(GATHERS[6])
+        weigh(UNITS[2])
+        gather(GATHERS[7])
+        weigh(UNITS[3])
         for h in range(PASSES):
             quantize_g(h, 0, 2)
+        turn_dy(UNITS[4])
+        turn_dy(UNITS[6])
         form_x(0, 0, PASSES)
+        turn_dy(UNITS[5])
         for unit in UNITS[4:6]:
-            turn_dy(unit)
             weigh(unit)
         quantize_x(0, 0, PASSES)
         quantize_g(0, 2, 4)
+        turn_dy(UNITS[7])
+        turn_gap(UNITS[7])
         for unit in UNITS[6:]:
-            turn_dy(unit)
             weigh(unit)
         form_x(1, 0, PASSES)
         quantize_x(1, 0, PASSES)
@@ -229,7 +242,7 @@ def tile_attend_gvq_s_w_kernel(tc, zT, cb, dyT, tw, xT, offs, out):
         quantize_x(2, 0, PASSES)
         for h in range(PASSES):
             quantize_x(LAST, h, h + 1)
-        accs = [banks.tile([P, DV], F32, name="bank") for b in range(BLOCKS)]
+        accs = [banks.tile([P, DV], F32, name="bank%d" % n) for n in (5, BANK[1, 1], BANK[2, 0], BANK[3, 0])]
         for b in range(BLOCKS):
             multiply(accs[b], b, 0)
         for b in range(BLOCKS):

@@ -15,6 +15,7 @@ U8 = mybir.dt.uint8
 E4M3X4 = mybir.dt.float8_e4m3fn_x4
 E5M2X4 = mybir.dt.float8_e5m2_x4
 MULT = mybir.AluOpType.mult
+ADD = mybir.AluOpType.add
 SUBTRACT = mybir.AluOpType.subtract
 
 P = 128
@@ -25,15 +26,11 @@ BLOCKS = DV // P
 LAST = BLOCKS - 1
 LIST_COLS = K_PASS // 16
 WINDOW = 2 * C
-X_BANKS = 2
-G_BANKS = 8 - X_BANKS
-
-
-UNITS = [(0, 0), (0, 1), (1, 0), (1, 1), (2, 0), (3, 0), (2, 1), (3, 1)]
-GATHERS = [(0, 0), (1, 0), (0, 1), (1, 1), (2, 0), (2, 1), (3, 0), (3, 1)]
-BANK = {(0, 0): 0, (1, 0): 1, (0, 1): 2, (1, 1): 3, (2, 0): 4, (2, 1): 0, (3, 0): 2, (3, 1): 1}
-EARLY = GATHERS[:2]
-LAID_OUT = 4
+UNITS = [(b, h) for b in range(BLOCKS) for h in range(PASSES)]
+EARLY = [(0, 0), (1, 0)]
+LAID = [(0, 1), (1, 1), (2, 0), (2, 1)]
+DIRECT = []
+BANK = {(0, 0): 0, (1, 0): 1, (0, 1): 2, (1, 1): 3, (2, 0): 4, (2, 1): 5, (3, 0): 0, (3, 1): 2}
 
 
 def tile_attend_gvq_s_w_kernel(tc, zT, cb, dyT, tw, xT, offs, out):
@@ -41,10 +38,9 @@ def tile_attend_gvq_s_w_kernel(tc, zT, cb, dyT, tw, xT, offs, out):
     with ExitStack() as ctx:
         keep = ctx.enter_context(tc.tile_pool(name="keep", bufs=1))
         banks = ctx.enter_context(tc.psum_pool(name="banks", bufs=1))
-        x_turn = ctx.enter_context(tc.psum_pool(name="x_turn", bufs=X_BANKS))
 
-        def unit_tiles(name, shape, dtype=F32):
-            return {(b, h): keep.tile(shape, dtype, name="%s%d%d" % (name, b, h)) for b, h in UNITS}
+        def unit_tiles(name, units, shape, dtype=F32):
+            return {u: keep.tile(shape, dtype, name="%s%d%d" % (name, u[0], u[1])) for u in units}
 
         offsets = keep.tile([P, T // 16], U16, name="offsets")
         books = [keep.tile([P, WINDOW], F32, name="book%d" % b) for b in range(BLOCKS)]
@@ -56,57 +52,67 @@ def tile_attend_gvq_s_w_kernel(tc, zT, cb, dyT, tw, xT, offs, out):
         def rows(b):
             return slice(b * P, (b + 1) * P)
 
-        def tokens(h):
-            return slice(h * K_PASS, (h + 1) * K_PASS)
+        def tokens(h0, h1=None):
+            return slice(h0 * K_PASS, (h0 + 1 if h1 is None else h1) * K_PASS)
 
         def load(tiles, source, b):
             nc.sync.dma_start(tiles[b][:, : source.shape[1]], source[rows(b), :])
 
+        def load_half(tiles, source, b, h):
+            nc.sync.dma_start(tiles[b][:, tokens(h)], source[rows(b), tokens(h)])
+
         load(books, cb, 0)
         nc.sync.dma_start(offsets[:], offs)
-        nc.sync.dma_start(tw_words[:], tw[0, :].rearrange("(h p j) -> p h j", h=PASSES, j=PACK))
         load(books, cb, 1)
         load(zs, zT, 0)
         load(zs, zT, 1)
+        nc.sync.dma_start(tw_words[:], tw[0, :].rearrange("(h p j) -> p h j", h=PASSES, j=PACK))
         load(books, cb, 2)
-        load(zs, zT, 2)
-        load(dys, dyT, 0)
+        load_half(zs, zT, 2, 0)
+        load_half(dys, dyT, 0, 0)
+        load_half(zs, zT, 2, 1)
+        load_half(dys, dyT, 0, 1)
         load(books, cb, 3)
+        load_half(zs, zT, 3, 0)
         load(dys, dyT, 1)
-        load(zs, zT, 3)
+        load_half(zs, zT, 3, 1)
         load(dys, dyT, 2)
-        load(xs, xT, 0)
         load(dys, dyT, 3)
+        load(xs, xT, 0)
         load(xs, xT, 1)
         load(xs, xT, 2)
-        for h in range(PASSES):
-            nc.sync.dma_start(xs[LAST][:, tokens(h)], xT[rows(LAST), tokens(h)])
+        load_half(xs, xT, 3, 0)
+        load_half(xs, xT, 3, 1)
 
         for b in range(BLOCKS):
             nc.vector.memset(books[b][:, C:], 0.0)
         ident = keep.tile([P, P], F32, name="ident")
         make_identity(nc, ident[:])
 
-        weights = keep.tile([P, PASSES, P, PACK], F32, name="weights")
+        weights = keep.tile([P, PASSES, PACK], F32, name="weights")
+        turned = [u for u in UNITS if u not in DIRECT]
+        gap_planes = unit_tiles("gap_planes", LAID, [P, PACK, P])
+        z_planes = unit_tiles("z_planes", EARLY, [P, PACK, P])
+        dy_planes = unit_tiles("dy_planes", turned, [P, PACK, P])
+        gaps = {u: t[:] for u, t in unit_tiles("gap", UNITS, [P, K_PASS]).items()}
 
-        def spread_weights(h):
-            nc.scalar.mul(weights[:, h], tw_words[:, h, :].unsqueeze(1).to_broadcast([P, P, PACK]), -BETA)
-
-        gap_planes = {unit: keep.tile([P, PACK, P], F32, name="gap_planes%d%d" % unit) for unit in GATHERS[:LAID_OUT]}
-        z_planes = {unit: keep.tile([P, PACK, P], F32, name="z_planes%d%d" % unit) for unit in EARLY}
-        dy_planes = unit_tiles("dy_planes", [P, PACK, P])
-        gaps = {unit: keep.tile([P, K_PASS], F32, name="gap%d%d" % unit)[:] for unit in GATHERS[:6]}
-        gaps[3, 0] = dy_planes[0, 1][:].rearrange("n j p -> n (j p)")
-        gaps[3, 1] = dy_planes[1, 0][:].rearrange("n j p -> n (j p)")
+        joined = unit_tiles("joined", DIRECT, [P, K_PASS])
+        g_words = unit_tiles("g_words", DIRECT, [P, K_PASS // 2])
         g_bf = keep.tile([P, PASSES, BLOCKS, P, PACK], BF16, name="g_bf", align_bytes=64)
         g_codes = keep.tile([P, PASSES, DV], U32, name="g_codes", align_bytes=64)
         g_scales = keep.tile([P, PASSES, DV], U8, name="g_scales", align_bytes=64)
-        x_words = [keep.tile([P, T // 2], F32, name="x_words%d" % b) for b in range(BLOCKS)]
+        x_words = [keep.tile([P, T // 2], F32, name="x_words%d" % b)[:] for b in range(BLOCKS)]
+
         x_bf = keep.tile([P, BLOCKS, T], BF16, name="x_bf", align_bytes=64)
         x_codes = keep.tile([P, BLOCKS, PASSES, P], U32, name="x_codes", align_bytes=64)
         x_scales = keep.tile([P, BLOCKS, PASSES, P], U8, name="x_scales", align_bytes=64)
         results = [keep.tile([P, DV], F32, name="result%d" % b) for b in range(BLOCKS)]
         sums = {}
+        accs = {}
+        x_banks = {}
+
+        def spread_weights(h):
+            nc.scalar.mul(weights[:, h], tw_words[:, h, :], -BETA)
 
         def gather(unit):
             b, h = unit
@@ -117,44 +123,41 @@ def tile_attend_gvq_s_w_kernel(tc, zT, cb, dyT, tw, xT, offs, out):
                 nc.vector.tensor_tensor(gaps[unit], picked, zs[b][:, tokens(h)], SUBTRACT)
 
         def lay_out(planes, values, factor):
-            nc.scalar.mul(planes[:].rearrange("n j p -> n p j"), values.rearrange("n (p j) -> n p j", j=PACK), factor)
-            return [planes[:, j, :] for j in range(PACK)]
+            halves = planes[:].rearrange("n j p -> n (j p)").rearrange("n (u p e) -> n u p e", u=2, e=2)
+            nc.scalar.mul(halves.rearrange("n u p e -> n p u e"), values.rearrange("n (p u e) -> n p u e", u=2, e=2), factor)
+            return [halves[:, j // 2, :, j % 2] for j in range(PACK)]
 
-        def add_planes(bank, planes, first, last):
+        def add_planes(unit, planes):
+            if unit not in sums:
+                sums[unit] = [banks.tile([P, PACK, P], F32, name="bank%d" % BANK[unit]), 0]
+            bank, done = sums[unit]
+            terms = 3 if unit in EARLY else 2
             for j in range(PACK):
                 nc.tensor.matmul(
                     bank[:, j, :],
                     planes[j],
                     ident[:],
-                    start=(first and j == 0),
-                    stop=(last and j == PACK - 1),
+                    start=(done == 0 and j == 0),
+                    stop=(done == terms - 1 and j == PACK - 1),
                     is_transpose=True,
                 )
-
-        def bank_of(unit):
-            first = unit not in sums
-            if first:
-                sums[unit] = banks.tile([P, PACK, P], F32, name="bank%d" % BANK[unit])
-            return sums[unit], first
+            sums[unit][1] = done + 1
 
         def turn_gap(unit):
-            b, h = unit
-            bank, first = bank_of(unit)
-            if unit in gap_planes:
-                add_planes(bank, lay_out(gap_planes[unit], gaps[unit], 1.0), first, not first)
+            if unit in LAID:
+                add_planes(unit, lay_out(gap_planes[unit], gaps[unit], 1.0))
             else:
-                add_planes(bank, [gaps[unit][:, j::PACK] for j in range(PACK)], first, not first)
-            if unit in EARLY:
-                add_planes(bank, lay_out(z_planes[unit], zs[b][:, tokens(h)], -1.0), False, False)
+                add_planes(unit, [gaps[unit][:, j::PACK] for j in range(PACK)])
+
+        def turn_z(unit):
+            add_planes(unit, lay_out(z_planes[unit], zs[unit[0]][:, tokens(unit[1])], -1.0))
 
         def turn_dy(unit):
-            b, h = unit
-            bank, first = bank_of(unit)
-            add_planes(bank, lay_out(dy_planes[unit], dys[b][:, tokens(h)], -1.0 / BETA), first, not first)
+            add_planes(unit, lay_out(dy_planes[unit], dys[unit[0]][:, tokens(unit[1])], -1.0 / BETA))
 
         def weigh(unit):
             b, h = unit
-            nc.vector.tensor_tensor(g_bf[:, h, b], sums[unit][:].rearrange("p j n -> p n j"), weights[:, h], MULT)
+            nc.vector.tensor_tensor(g_bf[:, h, b], sums[unit][0][:].rearrange("p j n -> p n j"), weights[:, h].unsqueeze(1).to_broadcast([P, P, PACK]), MULT)
 
         def quantize_g(h, b0, b1):
             cols = slice(b0 * P, b1 * P)
@@ -164,36 +167,36 @@ def tile_attend_gvq_s_w_kernel(tc, zT, cb, dyT, tw, xT, offs, out):
                 in_=g_bf[:, h, b0:b1].rearrange("p b n j -> p (b n j)"),
             )
 
-        def form_x(b, h0, h1):
+        def round_x(b, h0, h1, copy):
+            words = x_words[b][:, h0 * 2 * P : h1 * 2 * P]
+            copy(words.bitcast(BF16), xs[b][:, tokens(h0, h1)])
+
+        def turn_x(b, h0, h1, n):
             passes = h1 - h0
             words = x_words[b][:, h0 * 2 * P : h1 * 2 * P]
-            pairs = words.bitcast(BF16).rearrange("m (u p e) -> m p u e", u=2, e=2)
-            raw = xs[b][:, h0 * K_PASS : h1 * K_PASS].rearrange("m (p u e) -> m p u e", u=2, e=2)
-            if b < LAST:
-                nc.scalar.copy(pairs, raw)
-            else:
-                nc.vector.tensor_copy(pairs, raw)
-            bank = x_turn.tile([P, passes, 2, P], F32, name="x_bank")
+            bank = banks.tile([P, passes, 2, P], F32, name="bank%d" % n)
             for h in range(passes):
                 for u in range(2):
-                    first = (u * passes + h) * P
-                    nc.tensor.transpose(bank[:, h, u, :], words[:, first : first + P], ident[:])
-            grouped = x_bf[:, b, h0 * K_PASS : h1 * K_PASS].bitcast(F32)
-            nc.scalar.copy(
-                grouped.rearrange("p (h m u) -> p h m u", m=P, u=2),
-                bank[:].rearrange("p h u m -> p h m u"),
-            )
+                    nc.tensor.transpose(bank[:, h, u, :], words[:, h * 2 * P + u : (h + 1) * 2 * P : 2], ident[:])
+            x_banks[b, h0] = bank
+
+        def group_x(b, h0, h1, copy):
+            bank = x_banks[b, h0]
+            grouped = x_bf[:, b, tokens(h0, h1)].bitcast(F32)
+            copy(grouped.rearrange("p (h m u) -> p h m u", m=P, u=2), bank[:].rearrange("p h u m -> p h m u"))
 
         def quantize_x(b, h0, h1):
             nc.vector.quantize_mx(
                 out=x_codes[:, b, h0:h1, :].rearrange("p h m -> p (h m)").bitcast(E4M3X4),
                 scales=x_scales[:, b, h0:h1, :].rearrange("p h m -> p (h m)"),
-                in_=x_bf[:, b, h0 * K_PASS : h1 * K_PASS],
+                in_=x_bf[:, b, tokens(h0, h1)],
             )
 
-        def multiply(acc, b, h):
+        def multiply(b, h, n=None):
+            if h == 0:
+                accs[b] = banks.tile([P, DV], F32, name="bank%d" % n)
             nc.tensor.matmul_mx(
-                out=acc[:],
+                out=accs[b][:],
                 lhsT=x_codes[:, b, h, :].bitcast(E4M3X4),
                 lhsT_scale=x_scales[:, b, h, :],
                 rhs=g_codes[:, h, :].bitcast(E5M2X4),
@@ -202,53 +205,80 @@ def tile_attend_gvq_s_w_kernel(tc, zT, cb, dyT, tw, xT, offs, out):
                 stop=(h == PASSES - 1),
             )
 
-        for h in range(PASSES):
-            spread_weights(h)
-        for unit in GATHERS[:5]:
-            gather(unit)
-            turn_gap(unit)
-        gather(GATHERS[5])
-        for unit in UNITS[:2]:
-            turn_dy(unit)
-            weigh(unit)
-        turn_gap(GATHERS[5])
-        for unit in UNITS[2:4]:
-            turn_dy(unit)
-        gather(GATHERS[6])
-        turn_gap(GATHERS[6])
-        weigh(UNITS[2])
-        gather(GATHERS[7])
-        weigh(UNITS[3])
-        for h in range(PASSES):
-            quantize_g(h, 0, 2)
-        turn_dy(UNITS[4])
-        turn_dy(UNITS[6])
-        form_x(0, 0, PASSES)
-        turn_dy(UNITS[5])
-        for unit in UNITS[4:6]:
-            weigh(unit)
-        quantize_x(0, 0, PASSES)
-        quantize_g(0, 2, 4)
-        turn_dy(UNITS[7])
-        turn_gap(UNITS[7])
-        for unit in UNITS[6:]:
-            weigh(unit)
-        form_x(1, 0, PASSES)
-        quantize_x(1, 0, PASSES)
-        quantize_g(1, 2, 4)
-        form_x(2, 0, PASSES)
-        for h in range(PASSES):
-            form_x(LAST, h, h + 1)
-        quantize_x(2, 0, PASSES)
-        for h in range(PASSES):
-            quantize_x(LAST, h, h + 1)
-        accs = [banks.tile([P, DV], F32, name="bank%d" % n) for n in (5, BANK[1, 1], BANK[2, 0], BANK[3, 0])]
-        for b in range(BLOCKS):
-            multiply(accs[b], b, 0)
-        for b in range(BLOCKS):
-            multiply(accs[b], b, 1)
-            if b % 2 == 0:
-                nc.scalar.copy(results[b][:], accs[b][:])
-            else:
-                nc.vector.tensor_copy(results[b][:], accs[b][:])
+        def store(b, copy):
+            copy(results[b][:], accs[b][:])
             nc.sync.dma_start(out[rows(b), :], results[b][:])
+
+        on_s, on_v = nc.scalar.copy, nc.vector.tensor_copy
+        spread_weights(0)
+        spread_weights(1)
+        gather((0, 0))
+        turn_gap((0, 0))
+        turn_z((0, 0))
+        gather((1, 0))
+        turn_gap((1, 0))
+        turn_z((1, 0))
+        gather((0, 1))
+        turn_gap((0, 1))
+        gather((1, 1))
+        turn_gap((1, 1))
+        gather((2, 0))
+        turn_dy((0, 0))
+        turn_gap((2, 0))
+        gather((2, 1))
+        weigh((0, 0))
+        turn_dy((0, 1))
+        turn_gap((2, 1))
+        gather((3, 0))
+        weigh((0, 1))
+        turn_gap((3, 0))
+        turn_dy((1, 0))
+        turn_dy((1, 1))
+        gather((3, 1))
+        weigh((1, 0))
+        turn_gap((3, 1))
+        weigh((1, 1))
+        quantize_g(0, 0, 2)
+        quantize_g(1, 0, 2)
+        turn_dy((2, 0))
+        weigh((2, 0))
+        turn_dy((2, 1))
+        weigh((2, 1))
+        turn_dy((3, 0))
+        turn_dy((3, 1))
+        weigh((3, 0))
+        weigh((3, 1))
+        quantize_g(0, 2, 4)
+        quantize_g(1, 2, 4)
+        round_x(0, 0, 2, on_s)
+        turn_x(0, 0, 2, 6)
+        group_x(0, 0, 2, on_s)
+        round_x(1, 0, 2, on_s)
+        turn_x(1, 0, 2, 7)
+        group_x(1, 0, 2, on_s)
+        quantize_x(0, 0, 2)
+        multiply(0, 0, 4)
+        multiply(0, 1)
+        quantize_x(1, 0, 2)
+        round_x(2, 0, 2, on_v)
+        turn_x(2, 0, 2, 1)
+        group_x(2, 0, 2, on_s)
+        round_x(3, 0, 1, on_v)
+        turn_x(3, 0, 1, 3)
+        group_x(3, 0, 1, on_s)
+        round_x(3, 1, 2, on_v)
+        turn_x(3, 1, 2, 6)
+        group_x(3, 1, 2, on_s)
+        quantize_x(2, 0, 2)
+        quantize_x(3, 0, 1)
+        quantize_x(3, 1, 2)
+        store(0, on_v)
+        multiply(1, 0, 5)
+        multiply(1, 1)
+        store(1, on_s)
+        multiply(2, 0, 0)
+        multiply(2, 1)
+        store(2, on_v)
+        multiply(3, 0, 2)
+        multiply(3, 1)
+        store(3, on_s)

@@ -78,9 +78,12 @@ def tile_attend_gvq_s_w_kernel(tc, zT, cb, dyT, tw, xT, offs, out):
         load_half(zs, zT, 3, 1)
         load(dys, dyT, 2)
         load(dys, dyT, 3)
-        load(xs, xT, 0)
-        load(xs, xT, 1)
-        load(xs, xT, 2)
+        load_half(xs, xT, 0, 0)
+        load_half(xs, xT, 0, 1)
+        load_half(xs, xT, 1, 0)
+        load_half(xs, xT, 1, 1)
+        load_half(xs, xT, 2, 0)
+        load_half(xs, xT, 2, 1)
         load_half(xs, xT, 3, 0)
         load_half(xs, xT, 3, 1)
 
@@ -123,9 +126,8 @@ def tile_attend_gvq_s_w_kernel(tc, zT, cb, dyT, tw, xT, offs, out):
                 nc.vector.tensor_tensor(gaps[unit], picked, zs[b][:, tokens(h)], SUBTRACT)
 
         def lay_out(planes, values, factor):
-            halves = planes[:].rearrange("n j p -> n (j p)").rearrange("n (u p e) -> n u p e", u=2, e=2)
-            nc.scalar.mul(halves.rearrange("n u p e -> n p u e"), values.rearrange("n (p u e) -> n p u e", u=2, e=2), factor)
-            return [halves[:, j // 2, :, j % 2] for j in range(PACK)]
+            nc.scalar.mul(planes[:].rearrange("n j p -> n p j"), values.rearrange("n (p j) -> n p j", j=PACK), factor)
+            return [planes[:, j, :] for j in range(PACK)]
 
         def add_planes(unit, planes):
             if unit not in sums:
@@ -169,7 +171,8 @@ def tile_attend_gvq_s_w_kernel(tc, zT, cb, dyT, tw, xT, offs, out):
 
         def round_x(b, h0, h1, copy):
             words = x_words[b][:, h0 * 2 * P : h1 * 2 * P]
-            copy(words.bitcast(BF16), xs[b][:, tokens(h0, h1)])
+            pairs = words.bitcast(BF16).rearrange("m (u p e) -> m p u e", u=2, e=2)
+            copy(pairs, xs[b][:, tokens(h0, h1)].rearrange("m (p u e) -> m p u e", u=2, e=2))
 
         def turn_x(b, h0, h1, n):
             passes = h1 - h0
@@ -177,7 +180,8 @@ def tile_attend_gvq_s_w_kernel(tc, zT, cb, dyT, tw, xT, offs, out):
             bank = banks.tile([P, passes, 2, P], F32, name="bank%d" % n)
             for h in range(passes):
                 for u in range(2):
-                    nc.tensor.transpose(bank[:, h, u, :], words[:, h * 2 * P + u : (h + 1) * 2 * P : 2], ident[:])
+                    first = (u * passes + h) * P
+                    nc.tensor.transpose(bank[:, h, u, :], words[:, first : first + P], ident[:])
             x_banks[b, h0] = bank
 
         def group_x(b, h0, h1, copy):
@@ -250,28 +254,40 @@ def tile_attend_gvq_s_w_kernel(tc, zT, cb, dyT, tw, xT, offs, out):
         weigh((3, 1))
         quantize_g(0, 2, 4)
         quantize_g(1, 2, 4)
-        round_x(0, 0, 2, on_s)
-        turn_x(0, 0, 2, 6)
-        group_x(0, 0, 2, on_s)
-        round_x(1, 0, 2, on_s)
-        turn_x(1, 0, 2, 7)
-        group_x(1, 0, 2, on_s)
-        quantize_x(0, 0, 2)
+        round_x(0, 0, 1, on_s)
+        turn_x(0, 0, 1, 6)
+        group_x(0, 0, 1, on_s)
+        quantize_x(0, 0, 1)
+        round_x(0, 1, 2, on_v)
+        turn_x(0, 1, 2, 7)
+        group_x(0, 1, 2, on_s)
+        quantize_x(0, 1, 2)
+        round_x(1, 0, 1, on_s)
+        turn_x(1, 0, 1, 1)
+        group_x(1, 0, 1, on_s)
+        quantize_x(1, 0, 1)
+        round_x(1, 1, 2, on_v)
+        turn_x(1, 1, 2, 3)
+        group_x(1, 1, 2, on_s)
+        quantize_x(1, 1, 2)
+        round_x(2, 0, 1, on_s)
+        turn_x(2, 0, 1, 6)
+        group_x(2, 0, 1, on_s)
+        quantize_x(2, 0, 1)
+        round_x(2, 1, 2, on_v)
+        turn_x(2, 1, 2, 7)
+        group_x(2, 1, 2, on_s)
+        quantize_x(2, 1, 2)
+        round_x(3, 0, 1, on_s)
+        turn_x(3, 0, 1, 1)
+        group_x(3, 0, 1, on_s)
+        quantize_x(3, 0, 1)
+        round_x(3, 1, 2, on_v)
+        turn_x(3, 1, 2, 3)
+        group_x(3, 1, 2, on_s)
+        quantize_x(3, 1, 2)
         multiply(0, 0, 4)
         multiply(0, 1)
-        quantize_x(1, 0, 2)
-        round_x(2, 0, 2, on_v)
-        turn_x(2, 0, 2, 1)
-        group_x(2, 0, 2, on_s)
-        round_x(3, 0, 1, on_v)
-        turn_x(3, 0, 1, 3)
-        group_x(3, 0, 1, on_s)
-        round_x(3, 1, 2, on_v)
-        turn_x(3, 1, 2, 6)
-        group_x(3, 1, 2, on_s)
-        quantize_x(2, 0, 2)
-        quantize_x(3, 0, 1)
-        quantize_x(3, 1, 2)
         store(0, on_v)
         multiply(1, 0, 5)
         multiply(1, 1)

@@ -15,7 +15,6 @@ U8 = mybir.dt.uint8
 E4M3X4 = mybir.dt.float8_e4m3fn_x4
 E5M2X4 = mybir.dt.float8_e5m2_x4
 MULT = mybir.AluOpType.mult
-ADD = mybir.AluOpType.add
 SUBTRACT = mybir.AluOpType.subtract
 
 P = 128
@@ -23,14 +22,18 @@ PACK = 4
 K_PASS = P * PACK
 PASSES = T // K_PASS
 BLOCKS = DV // P
-LAST = BLOCKS - 1
-LIST_COLS = K_PASS // 16
+LIST_GROUP = 16
+LIST_COLS = K_PASS // LIST_GROUP
 WINDOW = 2 * C
+PAIR = 2
+MX_ALIGN = 64
+
 UNITS = [(b, h) for b in range(BLOCKS) for h in range(PASSES)]
 EARLY = [(0, 0), (1, 0)]
 LAID = [(0, 1), (1, 1), (2, 0), (2, 1)]
-DIRECT = []
-BANK = {(0, 0): 0, (1, 0): 1, (0, 1): 2, (1, 1): 3, (2, 0): 4, (2, 1): 5, (3, 0): 0, (3, 1): 2}
+G_BANK = {(0, 0): 0, (1, 0): 1, (0, 1): 2, (1, 1): 3, (2, 0): 4, (2, 1): 5, (3, 0): 0, (3, 1): 2}
+X_BANKS = [6, 7, G_BANK[1, 0], G_BANK[1, 1]]
+OUT_BANKS = [G_BANK[2, 0], G_BANK[2, 1], G_BANK[3, 0], G_BANK[3, 1]]
 
 
 def tile_attend_gvq_s_w_kernel(tc, zT, cb, dyT, tw, xT, offs, out):
@@ -39,26 +42,29 @@ def tile_attend_gvq_s_w_kernel(tc, zT, cb, dyT, tw, xT, offs, out):
         keep = ctx.enter_context(tc.tile_pool(name="keep", bufs=1))
         banks = ctx.enter_context(tc.psum_pool(name="banks", bufs=1))
 
-        def unit_tiles(name, units, shape, dtype=F32):
-            return {u: keep.tile(shape, dtype, name="%s%d%d" % (name, u[0], u[1])) for u in units}
+        def unit_tiles(name, units, shape):
+            return {u: keep.tile(shape, F32, name="%s%d%d" % (name, u[0], u[1])) for u in units}
 
-        offsets = keep.tile([P, T // 16], U16, name="offsets")
+        def bank_tile(n, shape):
+            return banks.tile(shape, F32, name="bank%d" % n)
+
+        def rows(b):
+            return slice(b * P, (b + 1) * P)
+
+        def tokens(h):
+            return slice(h * K_PASS, (h + 1) * K_PASS)
+
+        offsets = keep.tile([P, T // LIST_GROUP], U16, name="offsets")
         books = [keep.tile([P, WINDOW], F32, name="book%d" % b) for b in range(BLOCKS)]
         zs = [keep.tile([P, T], F32, name="z%d" % b) for b in range(BLOCKS)]
         dys = [keep.tile([P, T], F32, name="dy%d" % b) for b in range(BLOCKS)]
         xs = [keep.tile([P, T], F32, name="x%d" % b) for b in range(BLOCKS)]
         tw_words = keep.tile([P, PASSES, PACK], F32, name="tw_words")
 
-        def rows(b):
-            return slice(b * P, (b + 1) * P)
-
-        def tokens(h0, h1=None):
-            return slice(h0 * K_PASS, (h0 + 1 if h1 is None else h1) * K_PASS)
-
         def load(tiles, source, b):
             nc.sync.dma_start(tiles[b][:, : source.shape[1]], source[rows(b), :])
 
-        def load_half(tiles, source, b, h):
+        def load_pass(tiles, source, b, h):
             nc.sync.dma_start(tiles[b][:, tokens(h)], source[rows(b), tokens(h)])
 
         load(books, cb, 0)
@@ -68,24 +74,17 @@ def tile_attend_gvq_s_w_kernel(tc, zT, cb, dyT, tw, xT, offs, out):
         load(zs, zT, 1)
         nc.sync.dma_start(tw_words[:], tw[0, :].rearrange("(h p j) -> p h j", h=PASSES, j=PACK))
         load(books, cb, 2)
-        load_half(zs, zT, 2, 0)
-        load_half(dys, dyT, 0, 0)
-        load_half(zs, zT, 2, 1)
-        load_half(dys, dyT, 0, 1)
+        for h in range(PASSES):
+            load_pass(zs, zT, 2, h)
+            load_pass(dys, dyT, 0, h)
         load(books, cb, 3)
-        load_half(zs, zT, 3, 0)
+        load_pass(zs, zT, 3, 0)
         load(dys, dyT, 1)
-        load_half(zs, zT, 3, 1)
+        load_pass(zs, zT, 3, 1)
         load(dys, dyT, 2)
         load(dys, dyT, 3)
-        load_half(xs, xT, 0, 0)
-        load_half(xs, xT, 0, 1)
-        load_half(xs, xT, 1, 0)
-        load_half(xs, xT, 1, 1)
-        load_half(xs, xT, 2, 0)
-        load_half(xs, xT, 2, 1)
-        load_half(xs, xT, 3, 0)
-        load_half(xs, xT, 3, 1)
+        for b, h in UNITS:
+            load_pass(xs, xT, b, h)
 
         for b in range(BLOCKS):
             nc.vector.memset(books[b][:, C:], 0.0)
@@ -93,139 +92,124 @@ def tile_attend_gvq_s_w_kernel(tc, zT, cb, dyT, tw, xT, offs, out):
         make_identity(nc, ident[:])
 
         weights = keep.tile([P, PASSES, PACK], F32, name="weights")
-        turned = [u for u in UNITS if u not in DIRECT]
         gap_planes = unit_tiles("gap_planes", LAID, [P, PACK, P])
         z_planes = unit_tiles("z_planes", EARLY, [P, PACK, P])
-        dy_planes = unit_tiles("dy_planes", turned, [P, PACK, P])
-        gaps = {u: t[:] for u, t in unit_tiles("gap", UNITS, [P, K_PASS]).items()}
-
-        joined = unit_tiles("joined", DIRECT, [P, K_PASS])
-        g_words = unit_tiles("g_words", DIRECT, [P, K_PASS // 2])
-        g_bf = keep.tile([P, PASSES, BLOCKS, P, PACK], BF16, name="g_bf", align_bytes=64)
-        g_codes = keep.tile([P, PASSES, DV], U32, name="g_codes", align_bytes=64)
-        g_scales = keep.tile([P, PASSES, DV], U8, name="g_scales", align_bytes=64)
-        x_words = [keep.tile([P, T // 2], F32, name="x_words%d" % b)[:] for b in range(BLOCKS)]
-
-        x_bf = keep.tile([P, BLOCKS, T], BF16, name="x_bf", align_bytes=64)
-        x_codes = keep.tile([P, BLOCKS, PASSES, P], U32, name="x_codes", align_bytes=64)
-        x_scales = keep.tile([P, BLOCKS, PASSES, P], U8, name="x_scales", align_bytes=64)
+        dy_planes = unit_tiles("dy_planes", UNITS, [P, PACK, P])
+        gaps = unit_tiles("gap", UNITS, [P, K_PASS])
+        g_bf = keep.tile([P, PASSES, BLOCKS, P, PACK], BF16, name="g_bf", align_bytes=MX_ALIGN)
+        g_codes = keep.tile([P, PASSES, DV], U32, name="g_codes", align_bytes=MX_ALIGN)
+        g_scales = keep.tile([P, PASSES, DV], U8, name="g_scales", align_bytes=MX_ALIGN)
+        x_words = [keep.tile([P, T // PAIR], F32, name="x_words%d" % b) for b in range(BLOCKS)]
+        x_bf = keep.tile([P, BLOCKS, T], BF16, name="x_bf", align_bytes=MX_ALIGN)
+        x_codes = keep.tile([P, BLOCKS, PASSES, P], U32, name="x_codes", align_bytes=MX_ALIGN)
+        x_scales = keep.tile([P, BLOCKS, PASSES, P], U8, name="x_scales", align_bytes=MX_ALIGN)
         results = [keep.tile([P, DV], F32, name="result%d" % b) for b in range(BLOCKS)]
         sums = {}
-        accs = {}
-        x_banks = {}
-
-        def spread_weights(h):
-            nc.scalar.mul(weights[:, h], tw_words[:, h, :], -BETA)
+        terms_done = {}
 
         def gather(unit):
             b, h = unit
             picked = books[b][:].indirect(offsets[:, h * LIST_COLS : (h + 1) * LIST_COLS])
             if unit in EARLY:
-                nc.vector.tensor_copy(gaps[unit], picked)
+                nc.vector.tensor_copy(gaps[unit][:], picked)
             else:
-                nc.vector.tensor_tensor(gaps[unit], picked, zs[b][:, tokens(h)], SUBTRACT)
+                nc.vector.tensor_tensor(gaps[unit][:], picked, zs[b][:, tokens(h)], SUBTRACT)
 
         def lay_out(planes, values, factor):
-            nc.scalar.mul(planes[:].rearrange("n j p -> n p j"), values.rearrange("n (p j) -> n p j", j=PACK), factor)
+            nc.scalar.mul(
+                planes[:].rearrange("n j p -> n p j"), values.rearrange("n (p j) -> n p j", j=PACK), factor
+            )
             return [planes[:, j, :] for j in range(PACK)]
 
         def add_planes(unit, planes):
             if unit not in sums:
-                sums[unit] = [banks.tile([P, PACK, P], F32, name="bank%d" % BANK[unit]), 0]
-            bank, done = sums[unit]
+                sums[unit] = bank_tile(G_BANK[unit], [P, PACK, P])
+                terms_done[unit] = 0
             terms = 3 if unit in EARLY else 2
             for j in range(PACK):
                 nc.tensor.matmul(
-                    bank[:, j, :],
+                    sums[unit][:, j, :],
                     planes[j],
                     ident[:],
-                    start=(done == 0 and j == 0),
-                    stop=(done == terms - 1 and j == PACK - 1),
+                    start=(terms_done[unit] == 0 and j == 0),
+                    stop=(terms_done[unit] == terms - 1 and j == PACK - 1),
                     is_transpose=True,
                 )
-            sums[unit][1] = done + 1
+            terms_done[unit] += 1
 
         def turn_gap(unit):
             if unit in LAID:
-                add_planes(unit, lay_out(gap_planes[unit], gaps[unit], 1.0))
+                add_planes(unit, lay_out(gap_planes[unit], gaps[unit][:], 1.0))
             else:
                 add_planes(unit, [gaps[unit][:, j::PACK] for j in range(PACK)])
 
         def turn_z(unit):
-            add_planes(unit, lay_out(z_planes[unit], zs[unit[0]][:, tokens(unit[1])], -1.0))
+            b, h = unit
+            add_planes(unit, lay_out(z_planes[unit], zs[b][:, tokens(h)], -1.0))
 
         def turn_dy(unit):
-            add_planes(unit, lay_out(dy_planes[unit], dys[unit[0]][:, tokens(unit[1])], -1.0 / BETA))
+            b, h = unit
+            add_planes(unit, lay_out(dy_planes[unit], dys[b][:, tokens(h)], -1.0 / BETA))
 
         def weigh(unit):
             b, h = unit
-            nc.vector.tensor_tensor(g_bf[:, h, b], sums[unit][0][:].rearrange("p j n -> p n j"), weights[:, h].unsqueeze(1).to_broadcast([P, P, PACK]), MULT)
+            nc.vector.tensor_tensor(
+                g_bf[:, h, b],
+                sums[unit][:].rearrange("p j n -> p n j"),
+                weights[:, h].unsqueeze(1).to_broadcast([P, P, PACK]),
+                MULT,
+            )
 
-        def quantize_g(h, b0, b1):
+        def quantize_g(b0, b1):
             cols = slice(b0 * P, b1 * P)
-            nc.vector.quantize_mx(
-                out=g_codes[:, h, cols].bitcast(E5M2X4),
-                scales=g_scales[:, h, cols],
-                in_=g_bf[:, h, b0:b1].rearrange("p b n j -> p (b n j)"),
+            for h in range(PASSES):
+                nc.vector.quantize_mx(
+                    out=g_codes[:, h, cols].bitcast(E5M2X4),
+                    scales=g_scales[:, h, cols],
+                    in_=g_bf[:, h, b0:b1].rearrange("p b n j -> p (b n j)"),
+                )
+
+        def quantize_x(unit, n, round_with):
+            b, h = unit
+            words = x_words[b][:, h * PAIR * P : (h + 1) * PAIR * P]
+            round_with(
+                words.bitcast(BF16).rearrange("m (u p e) -> m p u e", u=PAIR, e=PAIR),
+                xs[b][:, tokens(h)].rearrange("m (p u e) -> m p u e", u=PAIR, e=PAIR),
             )
-
-        def round_x(b, h0, h1, copy):
-            words = x_words[b][:, h0 * 2 * P : h1 * 2 * P]
-            pairs = words.bitcast(BF16).rearrange("m (u p e) -> m p u e", u=2, e=2)
-            copy(pairs, xs[b][:, tokens(h0, h1)].rearrange("m (p u e) -> m p u e", u=2, e=2))
-
-        def turn_x(b, h0, h1, n):
-            passes = h1 - h0
-            words = x_words[b][:, h0 * 2 * P : h1 * 2 * P]
-            bank = banks.tile([P, passes, 2, P], F32, name="bank%d" % n)
-            for h in range(passes):
-                for u in range(2):
-                    first = (u * passes + h) * P
-                    nc.tensor.transpose(bank[:, h, u, :], words[:, first : first + P], ident[:])
-            x_banks[b, h0] = bank
-
-        def group_x(b, h0, h1, copy):
-            bank = x_banks[b, h0]
-            grouped = x_bf[:, b, tokens(h0, h1)].bitcast(F32)
-            copy(grouped.rearrange("p (h m u) -> p h m u", m=P, u=2), bank[:].rearrange("p h u m -> p h m u"))
-
-        def quantize_x(b, h0, h1):
-            nc.vector.quantize_mx(
-                out=x_codes[:, b, h0:h1, :].rearrange("p h m -> p (h m)").bitcast(E4M3X4),
-                scales=x_scales[:, b, h0:h1, :].rearrange("p h m -> p (h m)"),
-                in_=x_bf[:, b, tokens(h0, h1)],
+            bank = bank_tile(n, [P, PAIR, P])
+            for u in range(PAIR):
+                nc.tensor.transpose(bank[:, u, :], words[:, u * P : (u + 1) * P], ident[:])
+            grouped = x_bf[:, b, tokens(h)]
+            nc.scalar.copy(
+                grouped.bitcast(F32).rearrange("p (m u) -> p m u", u=PAIR), bank[:].rearrange("p u m -> p m u")
             )
+            nc.vector.quantize_mx(out=x_codes[:, b, h, :].bitcast(E4M3X4), scales=x_scales[:, b, h, :], in_=grouped)
 
-        def multiply(b, h, n=None):
-            if h == 0:
-                accs[b] = banks.tile([P, DV], F32, name="bank%d" % n)
-            nc.tensor.matmul_mx(
-                out=accs[b][:],
-                lhsT=x_codes[:, b, h, :].bitcast(E4M3X4),
-                lhsT_scale=x_scales[:, b, h, :],
-                rhs=g_codes[:, h, :].bitcast(E5M2X4),
-                rhs_scale=g_scales[:, h, :],
-                start=(h == 0),
-                stop=(h == PASSES - 1),
-            )
-
-        def store(b, copy):
-            copy(results[b][:], accs[b][:])
+        def multiply_and_store(b, copy):
+            acc = bank_tile(OUT_BANKS[b], [P, DV])
+            for h in range(PASSES):
+                nc.tensor.matmul_mx(
+                    out=acc[:],
+                    lhsT=x_codes[:, b, h, :].bitcast(E4M3X4),
+                    lhsT_scale=x_scales[:, b, h, :],
+                    rhs=g_codes[:, h, :].bitcast(E5M2X4),
+                    rhs_scale=g_scales[:, h, :],
+                    start=(h == 0),
+                    stop=(h == PASSES - 1),
+                )
+            copy(results[b][:], acc[:])
             nc.sync.dma_start(out[rows(b), :], results[b][:])
 
-        on_s, on_v = nc.scalar.copy, nc.vector.tensor_copy
-        spread_weights(0)
-        spread_weights(1)
-        gather((0, 0))
-        turn_gap((0, 0))
-        turn_z((0, 0))
-        gather((1, 0))
-        turn_gap((1, 0))
-        turn_z((1, 0))
-        gather((0, 1))
-        turn_gap((0, 1))
-        gather((1, 1))
-        turn_gap((1, 1))
+        for h in range(PASSES):
+            nc.scalar.mul(weights[:, h], tw_words[:, h, :], -BETA)
+
+        for unit in EARLY:
+            gather(unit)
+            turn_gap(unit)
+            turn_z(unit)
+        for unit in [(0, 1), (1, 1)]:
+            gather(unit)
+            turn_gap(unit)
         gather((2, 0))
         turn_dy((0, 0))
         turn_gap((2, 0))
@@ -242,59 +226,18 @@ def tile_attend_gvq_s_w_kernel(tc, zT, cb, dyT, tw, xT, offs, out):
         weigh((1, 0))
         turn_gap((3, 1))
         weigh((1, 1))
-        quantize_g(0, 0, 2)
-        quantize_g(1, 0, 2)
-        turn_dy((2, 0))
-        weigh((2, 0))
-        turn_dy((2, 1))
-        weigh((2, 1))
-        turn_dy((3, 0))
-        turn_dy((3, 1))
-        weigh((3, 0))
-        weigh((3, 1))
-        quantize_g(0, 2, 4)
-        quantize_g(1, 2, 4)
-        round_x(0, 0, 1, on_s)
-        turn_x(0, 0, 1, 6)
-        group_x(0, 0, 1, on_s)
-        quantize_x(0, 0, 1)
-        round_x(0, 1, 2, on_v)
-        turn_x(0, 1, 2, 7)
-        group_x(0, 1, 2, on_s)
-        quantize_x(0, 1, 2)
-        round_x(1, 0, 1, on_s)
-        turn_x(1, 0, 1, 1)
-        group_x(1, 0, 1, on_s)
-        quantize_x(1, 0, 1)
-        round_x(1, 1, 2, on_v)
-        turn_x(1, 1, 2, 3)
-        group_x(1, 1, 2, on_s)
-        quantize_x(1, 1, 2)
-        round_x(2, 0, 1, on_s)
-        turn_x(2, 0, 1, 6)
-        group_x(2, 0, 1, on_s)
-        quantize_x(2, 0, 1)
-        round_x(2, 1, 2, on_v)
-        turn_x(2, 1, 2, 7)
-        group_x(2, 1, 2, on_s)
-        quantize_x(2, 1, 2)
-        round_x(3, 0, 1, on_s)
-        turn_x(3, 0, 1, 1)
-        group_x(3, 0, 1, on_s)
-        quantize_x(3, 0, 1)
-        round_x(3, 1, 2, on_v)
-        turn_x(3, 1, 2, 3)
-        group_x(3, 1, 2, on_s)
-        quantize_x(3, 1, 2)
-        multiply(0, 0, 4)
-        multiply(0, 1)
-        store(0, on_v)
-        multiply(1, 0, 5)
-        multiply(1, 1)
-        store(1, on_s)
-        multiply(2, 0, 0)
-        multiply(2, 1)
-        store(2, on_v)
-        multiply(3, 0, 2)
-        multiply(3, 1)
-        store(3, on_s)
+        quantize_g(0, 2)
+        for h in range(PASSES):
+            turn_dy((2, h))
+            weigh((2, h))
+        for h in range(PASSES):
+            turn_dy((3, h))
+        for h in range(PASSES):
+            weigh((3, h))
+        quantize_g(2, BLOCKS)
+
+        rounders = [nc.scalar.copy, nc.vector.tensor_copy]
+        for i, unit in enumerate(UNITS):
+            quantize_x(unit, X_BANKS[i % len(X_BANKS)], rounders[unit[1]])
+        for b in range(BLOCKS):
+            multiply_and_store(b, nc.scalar.copy if b % 2 else nc.vector.tensor_copy)

@@ -31,6 +31,7 @@ MX_ALIGN = 64
 UNITS = [(b, h) for b in range(BLOCKS) for h in range(PASSES)]
 EARLY = [(0, 0), (1, 0)]
 LAID = [(0, 1), (1, 1), (2, 0), (2, 1)]
+SHARED_FROM = 2
 G_BANK = {(0, 0): 0, (1, 0): 1, (0, 1): 2, (1, 1): 3, (2, 0): 4, (2, 1): 5, (3, 0): 0, (3, 1): 2}
 X_BANKS = [6, 7, G_BANK[1, 0], G_BANK[1, 1]]
 OUT_BANKS = [G_BANK[2, 0], G_BANK[2, 1], G_BANK[3, 0], G_BANK[3, 1]]
@@ -236,8 +237,8 @@ def tile_attend_gvq_s_w_kernel(tc, zT, cb, dyT, tw, xT, offs, out):
             weigh((3, h))
         quantize_g(2, BLOCKS)
 
-        rounders = [nc.scalar.copy, nc.vector.tensor_copy]
-        for i, unit in enumerate(UNITS):
-            quantize_x(unit, X_BANKS[i % len(X_BANKS)], rounders[unit[1]])
+        for i, (b, h) in enumerate(UNITS):
+            round_with = nc.vector.tensor_copy if b >= SHARED_FROM and h == 1 else nc.scalar.copy
+            quantize_x((b, h), X_BANKS[i % len(X_BANKS)], round_with)
         for b in range(BLOCKS):
             multiply_and_store(b, nc.scalar.copy if b % 2 else nc.vector.tensor_copy)

@@ -16,6 +16,7 @@ E4M3X4 = mybir.dt.float8_e4m3fn_x4
 E5M2X4 = mybir.dt.float8_e5m2_x4
 MULT = mybir.AluOpType.mult
 SUBTRACT = mybir.AluOpType.subtract
+COPY = mybir.ActivationFunctionType.Copy
 
 P = 128
 PACK = 4
@@ -30,7 +31,7 @@ MX_ALIGN = 64
 
 UNITS = [(b, h) for b in range(BLOCKS) for h in range(PASSES)]
 EARLY = [(0, 0), (1, 0)]
-LAID = [(0, 1), (1, 1), (2, 0), (2, 1)]
+LAID = [(2, 0), (2, 1)]
 SHARED_FROM = 2
 G_BANK = {(0, 0): 0, (1, 0): 1, (0, 1): 2, (1, 1): 3, (2, 0): 4, (2, 1): 5, (3, 0): 0, (3, 1): 2}
 X_BANKS = [6, 7, G_BANK[1, 0], G_BANK[1, 1]]
@@ -69,15 +70,18 @@ def tile_attend_gvq_s_w_kernel(tc, zT, cb, dyT, tw, xT, offs, out):
             nc.sync.dma_start(tiles[b][:, tokens(h)], source[rows(b), tokens(h)])
 
         load(books, cb, 0)
-        nc.sync.dma_start(offsets[:], offs)
-        load(books, cb, 1)
-        load(zs, zT, 0)
-        load(zs, zT, 1)
         nc.sync.dma_start(tw_words[:], tw[0, :].rearrange("(h p j) -> p h j", h=PASSES, j=PACK))
+        nc.sync.dma_start(offsets[:], offs)
+        load_pass(zs, zT, 0, 1)
+        load(books, cb, 1)
+        load_pass(zs, zT, 1, 1)
         load(books, cb, 2)
-        for h in range(PASSES):
-            load_pass(zs, zT, 2, h)
-            load_pass(dys, dyT, 0, h)
+        load_pass(zs, zT, 2, 0)
+        load_pass(zs, zT, 0, 0)
+        load_pass(zs, zT, 2, 1)
+        load_pass(dys, dyT, 0, 0)
+        load_pass(zs, zT, 1, 0)
+        load_pass(dys, dyT, 0, 1)
         load(books, cb, 3)
         load_pass(zs, zT, 3, 0)
         load(dys, dyT, 1)
@@ -112,7 +116,7 @@ def tile_attend_gvq_s_w_kernel(tc, zT, cb, dyT, tw, xT, offs, out):
             b, h = unit
             picked = books[b][:].indirect(offsets[:, h * LIST_COLS : (h + 1) * LIST_COLS])
             if unit in EARLY:
-                nc.vector.tensor_copy(gaps[unit][:], picked)
+                nc.scalar.activation(gaps[unit][:], picked, COPY)
             else:
                 nc.vector.tensor_tensor(gaps[unit][:], picked, zs[b][:, tokens(h)], SUBTRACT)
 
@@ -201,19 +205,19 @@ def tile_attend_gvq_s_w_kernel(tc, zT, cb, dyT, tw, xT, offs, out):
             copy(results[b][:], acc[:])
             nc.sync.dma_start(out[rows(b), :], results[b][:])
 
-        for h in range(PASSES):
-            nc.scalar.mul(weights[:, h], tw_words[:, h, :], -BETA)
+        nc.scalar.mul(weights[:], tw_words[:], -BETA)
 
         for unit in EARLY:
             gather(unit)
             turn_gap(unit)
-            turn_z(unit)
         for unit in [(0, 1), (1, 1)]:
             gather(unit)
             turn_gap(unit)
+        turn_z((0, 0))
         gather((2, 0))
         turn_dy((0, 0))
         turn_gap((2, 0))
+        turn_z((1, 0))
         gather((2, 1))
         weigh((0, 0))
         turn_dy((0, 1))

@@ -190,20 +190,20 @@ def tile_attend_gvq_s_w_kernel(tc, zT, cb, dyT, tw, xT, offs, out):
             )
             nc.vector.quantize_mx(out=x_codes[:, b, h, :].bitcast(E4M3X4), scales=x_scales[:, b, h, :], in_=grouped)
 
-        def multiply_and_store(b, copy):
-            acc = bank_tile(OUT_BANKS[b], [P, DV])
+        def multiply_and_store(b, n, cols, copy):
+            acc = bank_tile(n, [P, cols.stop - cols.start])
             for h in range(PASSES):
                 nc.tensor.matmul_mx(
                     out=acc[:],
                     lhsT=x_codes[:, b, h, :].bitcast(E4M3X4),
                     lhsT_scale=x_scales[:, b, h, :],
-                    rhs=g_codes[:, h, :].bitcast(E5M2X4),
-                    rhs_scale=g_scales[:, h, :],
+                    rhs=g_codes[:, h, cols].bitcast(E5M2X4),
+                    rhs_scale=g_scales[:, h, cols],
                     start=(h == 0),
                     stop=(h == PASSES - 1),
                 )
-            copy(results[b][:], acc[:])
-            nc.sync.dma_start(out[rows(b), :], results[b][:])
+            copy(results[b][:, cols], acc[:])
+            nc.sync.dma_start(out[rows(b), cols], results[b][:, cols])
 
         nc.scalar.mul(weights[:], tw_words[:], -BETA)
 
@@ -244,5 +244,7 @@ def tile_attend_gvq_s_w_kernel(tc, zT, cb, dyT, tw, xT, offs, out):
         for i, (b, h) in enumerate(UNITS):
             round_with = nc.vector.tensor_copy if b >= SHARED_FROM and h == 1 else nc.scalar.copy
             quantize_x((b, h), X_BANKS[i % len(X_BANKS)], round_with)
-        for b in range(BLOCKS):
-            multiply_and_store(b, nc.scalar.copy if b % 2 else nc.vector.tensor_copy)
+        for b in range(BLOCKS - 1):
+            multiply_and_store(b, OUT_BANKS[b], slice(0, DV), nc.scalar.copy if b % 2 else nc.vector.tensor_copy)
+        multiply_and_store(BLOCKS - 1, OUT_BANKS[-1], slice(0, DV // 2), nc.scalar.copy)
+        multiply_and_store(BLOCKS - 1, X_BANKS[0], slice(DV // 2, DV), nc.vector.tensor_copy)

from contextlib import ExitStack

import concourse.mybir as mybir
from concourse.masks import make_identity

T, C, D, DV = 1024, 512, 512, 512
BETA = 0.25
FLOPS = 2 * D * DV * T

F32 = mybir.dt.float32
BF16 = mybir.dt.bfloat16
U32 = mybir.dt.uint32
U16 = mybir.dt.uint16
U8 = mybir.dt.uint8
E4M3X4 = mybir.dt.float8_e4m3fn_x4
E5M2X4 = mybir.dt.float8_e5m2_x4
MULT = mybir.AluOpType.mult
SUBTRACT = mybir.AluOpType.subtract
COPY = mybir.ActivationFunctionType.Copy

P = 128
PACK = 4
K_PASS = P * PACK
PASSES = T // K_PASS
BLOCKS = DV // P
LIST_GROUP = 16
LIST_COLS = K_PASS // LIST_GROUP
WINDOW = 2 * C
PAIR = 2
MX_ALIGN = 64

UNITS = [(b, h) for b in range(BLOCKS) for h in range(PASSES)]
EARLY = [(0, 0), (1, 0)]
LAID = [(2, 0), (2, 1)]
SHARED_FROM = 2
G_BANK = {(0, 0): 0, (1, 0): 1, (0, 1): 2, (1, 1): 3, (2, 0): 4, (2, 1): 5, (3, 0): 0, (3, 1): 2}
X_BANKS = [6, 7, G_BANK[1, 0], G_BANK[1, 1]]
OUT_BANKS = [G_BANK[2, 0], G_BANK[2, 1], G_BANK[3, 0], G_BANK[3, 1]]


def tile_attend_gvq_s_w_kernel(tc, zT, cb, dyT, tw, xT, offs, out):
    nc = tc.nc
    with ExitStack() as ctx:
        keep = ctx.enter_context(tc.tile_pool(name="keep", bufs=1))
        banks = ctx.enter_context(tc.psum_pool(name="banks", bufs=1))

        def unit_tiles(name, units, shape):
            return {u: keep.tile(shape, F32, name="%s%d%d" % (name, u[0], u[1])) for u in units}

        def bank_tile(n, shape):
            return banks.tile(shape, F32, name="bank%d" % n)

        def rows(b):
            return slice(b * P, (b + 1) * P)

        def tokens(h):
            return slice(h * K_PASS, (h + 1) * K_PASS)

        offsets = keep.tile([P, T // LIST_GROUP], U16, name="offsets")
        books = [keep.tile([P, WINDOW], F32, name="book%d" % b) for b in range(BLOCKS)]
        zs = [keep.tile([P, T], F32, name="z%d" % b) for b in range(BLOCKS)]
        dys = [keep.tile([P, T], F32, name="dy%d" % b) for b in range(BLOCKS)]
        xs = [keep.tile([P, T], F32, name="x%d" % b) for b in range(BLOCKS)]
        tw_words = keep.tile([P, PASSES, PACK], F32, name="tw_words")

        def load(tiles, source, b):
            nc.sync.dma_start(tiles[b][:, : source.shape[1]], source[rows(b), :])

        def load_pass(tiles, source, b, h):
            nc.sync.dma_start(tiles[b][:, tokens(h)], source[rows(b), tokens(h)])

        load(books, cb, 0)
        nc.sync.dma_start(tw_words[:], tw[0, :].rearrange("(h p j) -> p h j", h=PASSES, j=PACK))
        nc.sync.dma_start(offsets[:], offs)
        load_pass(zs, zT, 0, 1)
        load(books, cb, 1)
        load_pass(zs, zT, 1, 1)
        load(books, cb, 2)
        load_pass(zs, zT, 2, 0)
        load_pass(zs, zT, 0, 0)
        load_pass(zs, zT, 2, 1)
        load_pass(dys, dyT, 0, 0)
        load_pass(zs, zT, 1, 0)
        load_pass(dys, dyT, 0, 1)
        load(books, cb, 3)
        load_pass(zs, zT, 3, 0)
        load(dys, dyT, 1)
        load_pass(zs, zT, 3, 1)
        load(dys, dyT, 2)
        load(dys, dyT, 3)
        for b, h in UNITS:
            load_pass(xs, xT, b, h)

        for b in range(BLOCKS):
            nc.vector.memset(books[b][:, C:], 0.0)
        ident = keep.tile([P, P], F32, name="ident")
        make_identity(nc, ident[:])

        weights = keep.tile([P, PASSES, PACK], F32, name="weights")
        gap_planes = unit_tiles("gap_planes", LAID, [P, PACK, P])
        z_planes = unit_tiles("z_planes", EARLY, [P, PACK, P])
        dy_planes = unit_tiles("dy_planes", UNITS, [P, PACK, P])
        gaps = unit_tiles("gap", UNITS, [P, K_PASS])
        g_bf = keep.tile([P, PASSES, BLOCKS, P, PACK], BF16, name="g_bf", align_bytes=MX_ALIGN)
        g_codes = keep.tile([P, PASSES, DV], U32, name="g_codes", align_bytes=MX_ALIGN)
        g_scales = keep.tile([P, PASSES, DV], U8, name="g_scales", align_bytes=MX_ALIGN)
        x_words = [keep.tile([P, T // PAIR], F32, name="x_words%d" % b) for b in range(BLOCKS)]
        x_bf = keep.tile([P, BLOCKS, T], BF16, name="x_bf", align_bytes=MX_ALIGN)
        x_codes = keep.tile([P, BLOCKS, PASSES, P], U32, name="x_codes", align_bytes=MX_ALIGN)
        x_scales = keep.tile([P, BLOCKS, PASSES, P], U8, name="x_scales", align_bytes=MX_ALIGN)
        results = [keep.tile([P, DV], F32, name="result%d" % b) for b in range(BLOCKS)]
        sums = {}
        terms_done = {}

        def gather(unit):
            b, h = unit
            picked = books[b][:].indirect(offsets[:, h * LIST_COLS : (h + 1) * LIST_COLS])
            if unit in EARLY:
                nc.scalar.activation(gaps[unit][:], picked, COPY)
            else:
                nc.vector.tensor_tensor(gaps[unit][:], picked, zs[b][:, tokens(h)], SUBTRACT)

        def lay_out(planes, values, factor):
            nc.scalar.mul(
                planes[:].rearrange("n j p -> n p j"), values.rearrange("n (p j) -> n p j", j=PACK), factor
            )
            return [planes[:, j, :] for j in range(PACK)]

        def add_planes(unit, planes):
            if unit not in sums:
                sums[unit] = bank_tile(G_BANK[unit], [P, PACK, P])
                terms_done[unit] = 0
            terms = 3 if unit in EARLY else 2
            for j in range(PACK):
                nc.tensor.matmul(
                    sums[unit][:, j, :],
                    planes[j],
                    ident[:],
                    start=(terms_done[unit] == 0 and j == 0),
                    stop=(terms_done[unit] == terms - 1 and j == PACK - 1),
                    is_transpose=True,
                )
            terms_done[unit] += 1

        def turn_gap(unit):
            if unit in LAID:
                add_planes(unit, lay_out(gap_planes[unit], gaps[unit][:], 1.0))
            else:
                add_planes(unit, [gaps[unit][:, j::PACK] for j in range(PACK)])

        def turn_z(unit):
            b, h = unit
            add_planes(unit, lay_out(z_planes[unit], zs[b][:, tokens(h)], -1.0))

        def turn_dy(unit):
            b, h = unit
            add_planes(unit, lay_out(dy_planes[unit], dys[b][:, tokens(h)], -1.0 / BETA))

        def weigh(unit):
            b, h = unit
            nc.vector.tensor_tensor(
                g_bf[:, h, b],
                sums[unit][:].rearrange("p j n -> p n j"),
                weights[:, h].unsqueeze(1).to_broadcast([P, P, PACK]),
                MULT,
            )

        def quantize_g(b0, b1):
            cols = slice(b0 * P, b1 * P)
            for h in range(PASSES):
                nc.vector.quantize_mx(
                    out=g_codes[:, h, cols].bitcast(E5M2X4),
                    scales=g_scales[:, h, cols],
                    in_=g_bf[:, h, b0:b1].rearrange("p b n j -> p (b n j)"),
                )

        def quantize_x(unit, n, round_with):
            b, h = unit
            words = x_words[b][:, h * PAIR * P : (h + 1) * PAIR * P]
            round_with(
                words.bitcast(BF16).rearrange("m (u p e) -> m p u e", u=PAIR, e=PAIR),
                xs[b][:, tokens(h)].rearrange("m (p u e) -> m p u e", u=PAIR, e=PAIR),
            )
            bank = bank_tile(n, [P, PAIR, P])
            for u in range(PAIR):
                nc.tensor.transpose(bank[:, u, :], words[:, u * P : (u + 1) * P], ident[:])
            grouped = x_bf[:, b, tokens(h)]
            nc.scalar.copy(
                grouped.bitcast(F32).rearrange("p (m u) -> p m u", u=PAIR), bank[:].rearrange("p u m -> p m u")
            )
            nc.vector.quantize_mx(out=x_codes[:, b, h, :].bitcast(E4M3X4), scales=x_scales[:, b, h, :], in_=grouped)

        def multiply_and_store(b, n, cols, copy):
            acc = bank_tile(n, [P, cols.stop - cols.start])
            for h in range(PASSES):
                nc.tensor.matmul_mx(
                    out=acc[:],
                    lhsT=x_codes[:, b, h, :].bitcast(E4M3X4),
                    lhsT_scale=x_scales[:, b, h, :],
                    rhs=g_codes[:, h, cols].bitcast(E5M2X4),
                    rhs_scale=g_scales[:, h, cols],
                    start=(h == 0),
                    stop=(h == PASSES - 1),
                )
            copy(results[b][:, cols], acc[:])
            nc.sync.dma_start(out[rows(b), cols], results[b][:, cols])

        nc.scalar.mul(weights[:], tw_words[:], -BETA)

        for unit in EARLY:
            gather(unit)
            turn_gap(unit)
        for unit in [(0, 1), (1, 1)]:
            gather(unit)
            turn_gap(unit)
        turn_z((0, 0))
        gather((2, 0))
        turn_dy((0, 0))
        turn_gap((2, 0))
        turn_z((1, 0))
        gather((2, 1))
        weigh((0, 0))
        turn_dy((0, 1))
        turn_gap((2, 1))
        gather((3, 0))
        weigh((0, 1))
        turn_gap((3, 0))
        turn_dy((1, 0))
        turn_dy((1, 1))
        gather((3, 1))
        weigh((1, 0))
        turn_gap((3, 1))
        weigh((1, 1))
        quantize_g(0, 2)
        for h in range(PASSES):
            turn_dy((2, h))
            weigh((2, h))
        for h in range(PASSES):
            turn_dy((3, h))
        for h in range(PASSES):
            weigh((3, h))
        quantize_g(2, BLOCKS)

        for i, (b, h) in enumerate(UNITS):
            round_with = nc.vector.tensor_copy if b >= SHARED_FROM and h == 1 else nc.scalar.copy
            quantize_x((b, h), X_BANKS[i % len(X_BANKS)], round_with)
        for b in range(BLOCKS - 1):
            multiply_and_store(b, OUT_BANKS[b], slice(0, DV), nc.scalar.copy if b % 2 else nc.vector.tensor_copy)
        multiply_and_store(BLOCKS - 1, OUT_BANKS[-1], slice(0, DV // 2), nc.scalar.copy)
        multiply_and_store(BLOCKS - 1, X_BANKS[0], slice(DV // 2, DV), nc.vector.tensor_copy)
